import numpy as np, ml_dtypes
CORES = [40,64,80,88,96,104,120,144]
N = 8
BF = ml_dtypes.bfloat16
def gentries(a):
    return np.ascontiguousarray(a.reshape(8, 16, -1).transpose(0, 2, 1)).reshape(8, -1)
def gtable(e):
    e = np.asarray(e); return np.ascontiguousarray(e.reshape(8, -1, 16).transpose(0, 2, 1)).reshape(128, -1).astype(np.int32)
A, H, S, ST, RO, R = 1024, 2048, 256, 5, 2, 10
def atoms(rng, reach):
    off = np.concatenate([np.arange(-reach, 0), np.arange(1, reach + 1)])
    ch = off[np.argsort(rng.random((8, A, 2 * reach)), axis=-1)[..., :16]]
    ch = ch * (rng.random((8, A, 1)) >= 0.03125)
    pos = (np.arange(A)[None, :, None] + ch) % A
    nb = np.zeros((8, 16, A), np.int64)
    for g in range(8):
        o = rng.permutation(A); nb[g][:, o] = o[pos[g]].T
    return nb
def parts(rng, reach=R):
    nb = atoms(rng, reach); e = rng.integers(0, 256, (N, 8, 16, H)); s0 = rng.integers(0, A, (N, 8, RO, S))
    return nb, e, s0, rng.integers(0, 256, (N, 8, 16, S)), rng.integers(70 * ST, 210 * ST, (N, 8, 16))
def layers(rng):
    m = (A - 1) // (2 * ST - 1); lay = rng.permutation(A - 1)[:m * (2 * ST - 1)].reshape(2 * ST - 1, m); nb = rng.integers(0, A, (16, A))
    nb[:8, lay[0]] = rng.choice(lay[1], (8, m)); nb[8:, lay[0]] = rng.choice(lay[ST], (8, m))
    for i in range(1, 2 * ST - 1):
        nb[:, lay[i]] = A - 1 if i in (ST - 1, 2 * ST - 2) else rng.choice(lay[i + 1], (16, m))
    return nb, lay[0]
def owned(rng):
    n = 2 * ST; free = np.ones(A, bool); taken = np.zeros(H, bool); c = np.zeros((S, n), np.int64)
    for j in range(S):
        for m in range(n):
            x = rng.permutation(np.flatnonzero(free)); hs = []
            if m >= 2: hs.append(place(c[j, m - 2], c[j, m - 1], x))
            if m == n - 1: hs += [place(c[j, m - 1], x, c[j, 0]), place(x, c[j, 0], c[j, 1])]
            good = np.ones(x.shape, bool)
            for a in range(len(hs)):
                good &= ~taken[hs[a]]
                for b in range(a): good &= hs[a] != hs[b]
            i = int(np.argmax(good)); c[j, m] = x[i]; free[x[i]] = False
            for h in hs: taken[h[i]] = True
    nb = rng.integers(0, A, (16, A)); nb[:8, c[:, 0]] = c[:, 1]; nb[8:, c[:, 0]] = c[:, n - 1]
    for m in range(1, ST):
        nb[:, c[:, m]] = c[:, m + 1]; nb[:, c[:, n - m]] = c[:, n - m - 1]
    return nb, c[:, 0]
def pack(nb, e, s0, q, th):
    return {"nb": np.repeat(nb.reshape(1, 128, A), N, axis=0).astype(np.int32), "ang": e.reshape(N, 128, H).astype(np.float32).astype(BF),
            "st": np.stack([gtable(a.reshape(8, -1)) for a in s0]), "q": q.reshape(N, 128, S).astype(np.float32).astype(BF), "th": th.reshape(N, 128, 1).astype(np.int32)}
def setup_inputs(rng):
    return pack(*parts(rng))
def setup_inputs_ties(rng):
    nb, e, s0, q, th = parts(rng); v = np.arange(A)[None, :]
    nb[0] = 8 * (v >> 3) + rng.integers(0, 8, (16, A)); e[:, 0] = rng.choice(np.array([0, 192, 255, 255, 255]), (N, 1, H)); q[:, 0] = 0
    e[:, 1] = 10 * rng.integers(0, 2, (N, 16, H)); q[:, 1] = 10 * rng.integers(0, 2, (N, 16, S)); th[:, 1] = 10 * rng.integers(1, ST + 1, (N, 16))
    e[:, 2] = rng.choice(np.array([0, 3, 4, 255]), (N, 1, H)); q[:, 2] = 4; th[:, 2] = rng.integers(255, 520, (N, 1))
    e[:, 3] = 7; q[:, 3] = rng.integers(0, 256, (N, 16, S)); th[:, 3] = 7 * rng.integers(3, 2 * ST, (N, 16))
    e[:, 4] = rng.choice(np.array([100, 156]), (N, 16, H)); q[:, 4] = 128
    e[:, 5] = e[:, 5] * rng.integers(0, 2, (N, 16, H))
    for r in range(N):
        for g, n in ((5, 9), (6, 8), (7, 16)): th[r, g] = np.where(rng.permutation(16) < n, 0, 4095)
    return pack(nb, e, s0, q, th)
def setup_inputs_repeats(rng):
    nb, e, s0, q, th = parts(rng, 8)
    s0[:, ::2] = rng.choice(np.array([0, A - 1, A // 2, 5]), (N, 4, RO, S))
    e[:, 1::2] = e[:1, 1::2].copy(); q[:, 2::4] = q[:, 2::4, :, :1].copy()
    return pack(nb, e, s0, q, th >> 1)
def setup_inputs_stuck(rng):
    nb, e, s0, q, th = parts(rng); v = np.arange(A)[None, :]; k = np.arange(16)[:, None]
    nb[0] = 4 * (v >> 2) + rng.integers(0, 4, (16, A))
    nb[1, :8] = v; nb[2, 8:] = v
    nb[3] = v ^ rng.integers(0, 2, (16, A)); nb[3, ::8] = v ^ 1; nb[4] = v
    nb[5] = nb[5][rng.integers(0, 4, (16, A)), np.repeat(v, 16, axis=0)]
    nb[6] = 8 * (v >> 3) + rng.integers(0, 8, (16, A))
    x = v & 127; nb[7] = np.where(x == 0, v + 16 + k, np.where((x < 16) | (x >= 16 * (ST - 2)), v - x, v + 16))
    for g in (0, 3, 4, 6): th[:, g] = rng.integers(0, 800, (N, 16))
    s0[:, :, :, 0] = 0; s0[:, :, :, S - 1] = A - 1
    s0[:, 7] = 128 * rng.integers(0, A >> 7, (N, RO, S)) + rng.integers(1, 16, (N, RO, S))
    s0[0, 3] = rng.integers(256, A, (RO, 1)); th[0, 3] = 0
    return pack(nb, e, s0, q, th)
def setup_inputs_far(rng):
    nb, e, s0, q, th = parts(rng)
    for g in range(8):
        nb[g], a = layers(rng); s0[:, g] = rng.choice(a, (N, RO, S))
    if 2 * ST * S <= A:
        nb[1], a = owned(rng); s0[:, 1] = a[np.argsort(rng.random((N, RO, S)), axis=-1)]
    th = rng.integers(200 * ST, 300 * ST, (N, 8, 16)); th[2:, 5] = 4095; th[2:, 6] = 0; th[:2] = 0
    e[:, 2] = rng.integers(224, 256, (N, 16, H)); th[:, 2] = rng.integers(min(2048, 448 * ST), 448 * ST + 1, (N, 16))
    e[:, 3] = 255; th[:, 3] = 510 * ST; th[2:, 3, :8] = 510 * ST + 1
    return pack(nb, e, s0, q, th)
def setup_inputs_spread(rng):
    nb, e, s0, q, th = parts(rng); v = np.arange(A)[None, :]; k = np.arange(16)[:, None]
    e = (np.exp2(8 * rng.random((N, 8, 1, H))) * rng.random((N, 8, 16, H))).astype(np.int64)
    q = (np.exp2(8 * rng.random((N, 8, 1, S))) * rng.random((N, 8, 16, S))).astype(np.int64)
    th = np.minimum(np.exp2(12 * rng.random((N, 8, 16))).astype(np.int64), 4095)
    s0 = np.minimum((A * rng.random((N, 8, RO, S)) ** 3).astype(np.int64), A - 1)
    c = v & 3; nb[0] = 4 * rng.integers(0, A >> 2, (16, A)) + np.where(c >= 2, c, np.where(k < 8, 2, 3))
    s0[:, 0] = 4 * (s0[:, 0] >> 2) + rng.integers(0, 2, (N, RO, S))
    nb[2:4] = rng.integers(0, A, (2, 16, A))
    return pack(nb, e, s0, q, th)
def check_inputs(d):
    bad = []
    for k, lo, hi in (("nb", 0, A - 1), ("ang", 0, 255), ("st", 0, A - 1), ("q", 0, 255), ("th", 0, 4095)):
        v = np.asarray(d[k]).astype(np.float64)
        if not np.all((v >= lo) & (v <= hi)): bad.append("range of " + k)
        elif not np.all(v == np.floor(v)): bad.append(k + " holds numbers that aren't whole")
    if np.any(d["nb"] != d["nb"][:1]): bad.append("nb isn't alike on all ranks")
    return bad
def place(p, v, n):
    return ((((2 * p + 1) * (2 * n + 1)) >> 4) + 37 * v) & (H - 1)
def walk(e, v0, w, rows, nbr):
    path = [v0]; kk = np.arange(16)[None, :, None]
    for i in range(ST):
        v = path[i]; p = path[max(i - 1, 0)]
        n = np.take_along_axis(nbr, v[:, None, :], 2)
        h = place(p[:, None, :], v[:, None, :], n)
        x = np.take_along_axis(e, h.reshape(8, 1, 16 * S), 2).reshape(8, 16, 16, S)
        sc = np.add.reduce(np.abs(x - w[:, :, None, :]), axis=1)
        bar = np.any(np.stack(path)[:, :, None, :] == n[None], axis=0)
        if i == 0: bar = bar | (kk < rows) | (kk >= rows + 8)
        sc = np.where(bar, 2 ** 20, sc); k = np.argmin(sc, axis=1)[:, None, :]
        ok = np.take_along_axis(sc, k, 1)[:, 0] < 2 ** 20
        path.append(np.where(ok, np.take_along_axis(n, k, 1)[:, 0], v))
    return np.stack(path)
def reference(nb, ang, st, q, th):
    e = np.asarray(ang, np.float32).astype(np.int32).reshape(N, 8, 16, H); w = np.asarray(q, np.float32).astype(np.int32).reshape(N, 8, 16, S)
    lim = th.astype(np.int64).reshape(N, 8, 16, 1); nbr = nb.astype(np.int64).reshape(N, 8, 16, A)
    sl = np.stack([gentries(a) for a in st]).astype(np.int64).reshape(N, 8, RO, S)
    rings = np.zeros((N, 8, 16, RO, S), np.int64); m = np.arange(16)[None, :, None]
    for t in range(RO):
        new = []
        for r in range(N):
            s = (r + 1 + t % (N - 1)) % N
            pa = walk(e[r], sl[r, :, t], w[r], 0, nbr[r]); pb = walk(e[s], sl[r, :, t], w[r], 8, nbr[s])
            eq = pa[1:, None] == pb[None, 1:]; eq[0, 0] = False
            eq = eq.reshape(ST * ST, 8, S); found = np.any(eq, axis=0); f = np.argmax(eq, axis=0)
            i = f // ST + 1; j = f - (i - 1) * ST + 1; ln = np.where(found, i + j, 0)[:, None, :]; i = i[:, None, :]
            ca = np.take_along_axis(pa.transpose(1, 0, 2), np.minimum(m, i), 1); cb = np.take_along_axis(pb.transpose(1, 0, 2), np.clip(ln - m, 0, ST), 1)
            c = np.where(m <= i, ca, cb); live = m < ln
            before = np.take_along_axis(c, np.clip(np.where(m == 0, ln - 1, m - 1), 0, 15), 1)
            after = np.take_along_axis(c, np.clip(np.where(m == ln - 1, 0, m + 1), 0, 15), 1)
            h = place(before, c, after)
            x = np.take_along_axis(e[r], h.reshape(8, 1, 16 * S), 2).reshape(8, 16, 16, S)
            tot = np.add.reduce(np.where(live[:, None], x, 0), axis=2)
            heavy = found & (np.add.reduce((tot >= lim[r]).astype(np.int64), axis=1) >= 9)
            use = live & heavy[:, None, :]; gg = np.broadcast_to(np.arange(8)[:, None, None], h.shape)
            mark = np.zeros((8, H), bool); mark[gg[use], h[use]] = True
            new.append(np.where(mark[:, None, :], e[r] - (e[r] >> 2), e[r])); rings[r, :, :, t] = np.where(live, c, -1)
        e = np.stack(new)
    return {"ye": e.reshape(N, 128, H).astype(np.float32).astype(BF), "yr": rings.reshape(N, 128, RO * S).astype(np.float32)}

@@ -1,0 +1,739 @@
+from concourse.mybir import dt, AluOpType, ActivationFunctionType
+import comms_topo
+
+OP = AluOpType
+FN = ActivationFunctionType
+BIG = float(2 ** 26)
+REST = float(2041 * 8192)
+F32, B16, H16, I32 = "float32", "bfloat16", "float16", "int32"
+SCRATCH = {}
+for _n, _p, _w, _t in (
+        ("NB", 128, 1024, I32), ("XI", 128, 1024, I32), ("TO", 128, 2064, B16), ("TO1", 128, 2064, B16), ("TO2", 128, 2048, B16),
+        ("TP0", 128, 2048, B16), ("TPn", 128, 2048, B16), ("TP1", 128, 2048, B16), ("EL0", 128, 2048, B16), ("ELn", 128, 2048, B16),
+        ("EL1", 128, 2048, B16), ("TMP", 128, 2048, H16), ("ST", 128, 32, I32), ("SU", 128, 32, "uint16"), ("TH", 128, 1, I32),
+        ("THF", 128, 1, F32), ("Q", 128, 256, B16), ("QR", 128, 4096, B16), ("ON", 128, 2048, B16), ("CB", 128, 1232, B16),
+        ("CT", 128, 336, B16), ("CH", 128, 1232, H16), ("CF", 9, 1024, B16), ("CW", 9, 1408, H16), ("VS", 8, 2048, B16),
+        ("VH", 8, 2048, H16), ("SELL", 128, 2048, B16), ("CBIG", 128, 256, B16), ("S8", 128, 8, B16), ("NEGI", 128, 128, B16),
+        ("CR", 33, 512, B16), ("I128", 128, 128, B16), ("THR", 128, 512, B16), ("RT", 80, 1280, B16), ("MT0", 128, 128, B16),
+        ("WT", 128, 384, B16), ("NT", 9, 3072, H16), ("X0B", 128, 256, H16), ("PT0", 128, 176, H16), ("PT1", 128, 176, H16),
+        ("NPK0", 128, 128, F32), ("NPK1", 128, 128, F32), ("U", 128, 176, F32), ("PR", 128, 144, F32), ("V5", 128, 144, F32),
+        ("TT", 128, 160, I32), ("HH", 128, 160, I32), ("EQ", 128, 384, B16), ("EW", 128, 384, B16), ("E1", 128, 192, B16),
+        ("E2", 128, 96, B16), ("E3", 128, 64, B16), ("JS", 128, 128, F32), ("JR", 128, 16, I32), ("IL", 128, 32, H16),
+        ("VV", 128, 176, F32), ("MI", 128, 160, F32), ("JP", 128, 240, H16), ("UJ", 128, 48, F32), ("WW", 128, 160, I32),
+        ("TB", 128, 160, I32), ("TBP", 128, 160, F32), ("TV", 128, 160, H16), ("TVL", 80, 256, B16), ("HS", 128, 160, F32),
+        ("HV", 128, 160, H16), ("WS", 128, 160, F32), ("HT", 80, 256, H16), ("OFR", 128, 256, "uint16"), ("XR", 128, 4096, B16),
+        ("CMP", 128, 256, B16), ("HVY", 80, 256, B16), ("TM", 80, 256, B16), ("OH", 128, 20480, B16), ("TL", 128, 2560, B16),
+        ("CS", 128, 132, F32), ("DD", 128, 128, F32), ("MK", 128, 128, B16), ("MKT", 128, 128, B16), ("MKP", 128, 128, B16),
+        ("YN", 128, 256, H16), ("YM", 128, 256, H16), ("YP", 128, 256, H16), ("YK", 128, 1024, H16), ("YB", 128, 1536, H16),
+        ("YR", 128, 512, F32)):
+    SCRATCH[_n] = ("sbuf", [_p, _w], _t)
+for _c in "01":
+    for _n, _w, _t in (("NN", 256, H16), ("M", 256, F32), ("T", 256, I32), ("B", 256, I32), ("OF", 256, "uint16"), ("DV", 2048, B16),
+                       ("AB", 4096, B16), ("XG", 2048, B16), ("BQ", 1280, B16), ("SB", 128, F32), ("L1", 128, F32), ("L2", 64, F32),
+                       ("K", 32, I32), ("KD", 64, F32), ("SH", 32, I32), ("R", 32, I32), ("VL", 16, "uint16")):
+        SCRATCH[_n + _c] = ("sbuf", [128, _w], _t)
+BANKS = ("kA", "kB", "wA", "wB", "xA", "xB", "dA", "dB")
+for _b in BANKS:
+    SCRATCH[_b] = ("psum", [128, 512], F32)
+NITEM = 7
+NDMA = 14
+SEMAPHORES = ["v", "s", "t", "gc", "aTP0", "aTPn", "aMK"] + ["d%d" % i for i in range(NDMA)]
+SEMAPHORES += ["ri%d" % i for i in range(NITEM)] + ["lo%d" % i for i in range(NITEM)]
+
+CY = 0.00104
+TCY = 0.00075
+LEAD = 6.0
+ORDERS = {}
+
+
+def items(x, T, topo):
+    me = T.cores[x]
+    n = len(T.cores)
+
+    def via(dst, other):
+        if not other and topo.may_write(me, dst):
+            return None
+        for c in topo.cores_of(me):
+            if c != me and topo.may_write(c, dst) and (topo.die(c) != topo.die(me)) == bool(other):
+                return c
+        for c in topo.cores_of(me):
+            if c != me and topo.may_write(c, dst):
+                return c
+        return None
+    out = []
+    d0, d1 = T.cores[(x - 1) % n], T.cores[(x - 2) % n]
+    for h, c0 in ((0, 0), (1, 1024), (0, 512), (1, 1536)):
+        out.append(("TO", c0, c0 + 512, "TP0", "aTP0", d0, via(d0, h)))
+    for h in (0, 1):
+        out.append(("TO", h * 1024, h * 1024 + 1024, "TPn", "aTPn", d1, via(d1, h)))
+    out.append(("MKT", 0, 128, "MKP", "aMK", d1, via(d1, 0)))
+    return out
+
+
+def remote(g, T, topo, core, dst, out, src, rsem, lsem):
+    rid, pid = topo.addr(dst, core)
+    g.remote_dma(out, src, T.sem[rsem], T.sem[lsem], pid, rid, topo.mask(core, dst))
+
+
+def hand_on(g, core, T, topo):
+    todo = []
+    for x in range(len(T.cores)):
+        for k, it in enumerate(items(x, T, topo)):
+            if it[6] == core:
+                todo.append((k, it, len(topo.engines(T.cores[x], core))))
+    for k, it, ne in todo:
+        g.wait_ge(T.sem["ri%d" % k], ne)
+        ap = T[it[3]][:, it[1]:it[2]]
+        remote(g, T, topo, core, it[5], ap, ap, it[4], "lo%d" % k)
+    for k, it, ne in todo:
+        g.wait_ge(T.sem["lo%d" % k], len(topo.engines(core, it[5])))
+
+
+def build(g, core, T, topo):
+    ops = []
+    lastw, reads, bank = {}, {}, {}
+    bon = [0.0]
+
+    def op(q, fn, R, W, cost, kind="c", sem=None, val=1, lat=0.0):
+        n = len(ops)
+        deps, order = set(), set()
+        for k in list(R) + list(W):
+            if k[0] == "#":
+                b = bank.setdefault(k, {})
+                for e in b:
+                    if e == q:
+                        order.add(b[e][-1])
+                    elif e != "last":
+                        deps.update(b[e])
+                b[q] = b[q] + [n] if b.get("last") == [q] else [n]
+                b["last"] = [q]
+        for k in R:
+            if k[0] != "#":
+                if k in lastw:
+                    deps.add(lastw[k])
+                reads.setdefault(k, []).append(n)
+        for k in W:
+            if k[0] != "#":
+                if k in lastw:
+                    deps.add(lastw[k])
+                deps.update(reads.get(k, []))
+                lastw[k] = n
+                reads[k] = []
+        deps.discard(n)
+        order.discard(n)
+        ops.append(dict(q=q, fn=fn, deps=deps, order=(order - deps if q == "t" else set()), cost=cost, lat=lat, kind=kind, sem=sem, val=val, bon=bon[0]))
+
+    def V(fn, R, W, n):
+        op("v", lambda: fn(g.vector), R, W, max(64, n) * CY + 0.03)
+
+    def TS(out, a, s1, o0, R, W, n, s2=None, o1=None):
+        if o1 is None:
+            V(lambda e: e.tensor_scalar(out, a, s1, None, o0), R, W, n)
+        else:
+            V(lambda e: e.tensor_scalar(out, a, s1, s2, o0, o1), R, W, n)
+
+    def TTo(out, a, b, o, R, W, n):
+        V(lambda e: e.tensor_tensor(out, a, b, o), R, W, n)
+
+    def CP(out, a, R, W, n):
+        V(lambda e: e.tensor_copy(out, a), R, W, n)
+
+    def fill(ap, c, R, W, n):
+        V(lambda e: e.memset(ap, c), R, W, n)
+
+    def S(out, a, f, R, W, n):
+        op("s", lambda: g.scalar.activation(out, a, f), R, W, max(64, n) * CY + 0.05)
+
+    def MM(out, l, r, st, sp, R, W, m, n):
+        op("t", lambda: g.tensor.matmul(out, l, r, st, sp), R, W, max(min(64, m), n) * TCY + 0.01)
+
+    def GC(fn, R, W, n):
+        op("g", fn, R, W, 0.18 + 2 * n * CY)
+
+    def iota(out, pat, base, R, W, n):
+        GC(lambda: g.iota(out, pat, base, 0, allow_small_or_imprecise_dtypes=True), R, W, n)
+
+    nd = [0]
+
+    def DMA(q, out, a, R, W):
+        s = "d%d" % nd[0]
+        nd[0] += 1
+        eng = g.sync if q == "y" else g.scalar
+        op(q, lambda: eng.dma_start(out, a), R, W, 0.06, "d", s, 16, 2.5)
+
+    PS = {b: T[b] for b in BANKS}
+
+    DMA("y", T.ST[:, :], T.st[:, :], [], ["ST"])
+    DMA("s", T.TO[:, 0:2048], T.ang[:, :], [], ["TO"])
+    DMA("y", T.NB[:, :], T.nb[:, :], [], ["NB"])
+    DMA("s", T.Q[:, :], T.q[:, :], [], ["Q"])
+    DMA("y", T.TH[:, :], T.th[:, :], [], ["TH"])
+
+    fill(T.ON[:, :], 1.0, [], ["ON"], 1024)
+    fill(T.TO[:, 2048:2064], 0.0, [], ["TOz"], 64)
+    fill(T.TO1[:, 2048:2064], 0.0, [], ["TO1z"], 64)
+
+    def aff(out, src, pat, cmp, fv, base, cm, R, W):
+        n = 1
+        for p in pat:
+            n *= p[1]
+        GC(lambda: g.affine_select(out, src, pat, cmp, fv, base, cm), R, W, n)
+
+    def eqs(b, c0, pat, base, key, rows=128, cm=1):
+        n = 1
+        for p in pat:
+            n *= p[1]
+        aff(b[0:rows, c0:c0 + n], T.ON[0:rows, 0:n], pat, OP.is_equal, 0.0, base, cm, ["ON"], [key])
+
+    GC(lambda: g.iota(T.XI[:, 0:256], [[1, 256]], 0, 0), [], ["XI0"], 256)
+    for z in range(1, 4):
+        TS(T.XI[:, z * 256:z * 256 + 256], T.XI[:, 0:256], float(z * 256), OP.add, ["XI0"], ["XI%d" % z], 256)
+    CB, CH, CF, CW, CT = T.CB, T.CH, T.CF, T.CW, T.CT
+    hi = [[0, 8], [1, 2], [0, 8]]
+    eqs(CB, 128, [[-1, 8], [-8, 2], [-16, 8]], 0, "cPM")
+    eqs(CB, 0, [[-1, 128]], 0, "cI")
+    iota(CT[:, 208:336], hi, 0, [], ["cHi"], 128)
+    eqs(CB, 256, [[-1, 8], [-16, 8]], 0, "cA1")
+    eqs(CB, 320, [[-1, 8], [-16, 8]], -8, "cB1")
+    eqs(CF, 384, [[-1, 8], [0, 16]], 0, "cE0", 9)
+    aff(CF[0:9, 0:128], CF[0:9, 384:512], [[0, 128]], OP.not_equal, 0.5, -8, 1, ["cE0"], ["cF0"])
+    for z, kz in ((0, "cF"), (384, "cE")):
+        TTo(CF[0:9, z + 256:z + 384], CF[0:9, z:z + 128], CT[0:9, 208:336], OP.mult, [kz + "0", "cHi"], [kz + "2"], 256)
+        TTo(CF[0:9, z + 128:z + 256], CF[0:9, z:z + 128], CF[0:9, z + 256:z + 384], OP.subtract, [kz + "0", kz + "2"], [kz + "1"], 256)
+    fill(T.CR[:, :], 0.0, [], ["CR"], 256)
+    fill(T.CR[0:1, :], -16711680.0, ["CR"], ["CR"], 256)
+    iota(T.CR[32:33, 0:256], [[0, 2], [1024, 8], [0, 16]], 0, ["CR"], ["CR"], 256)
+    for z in (256, 384):
+        iota(T.CR[32:33, z:z + 64], [[1024, 8], [0, 8]], 0, ["CR"], ["CR"], 64)
+    aff(CT[:, 0:128], T.ON[:, 0:128], [[-16, 8], [0, 16]], OP.is_ge, 0.0, 0, 1, ["ON"], ["cT0"])
+    aff(CB[:, 896:1024], CT[:, 0:128], [[16, 8], [0, 16]], OP.is_ge, 0.0, 15, -1, ["cT0"], ["cEB"])
+    eqs(T.VS, 0, [[1, 16], [-16, 8], [-1, 16]], 0, "VS", 8, 16)
+    iota(T.I128[:, :], [[1, 128]], -128, [], ["I128"], 128)
+    iota(T.THR[:, :], [[0, 32], [1, 16]], 2, [], ["THR"], 512)
+    eqs(T.RT, 0, [[-1, 80], [0, 16]], 0, "RT", 80)
+    iota(T.MT0[:, :], [[0, 8], [1, 16]], 0, [], ["MT0"], 128)
+    aff(CT[:, 128:208], T.ON[:, 0:80], [[0, 10], [-16, 8]], OP.is_ge, 0.0, 0, 1, ["ON"], ["cT1"])
+    aff(CB[:, 1024:1104], CT[:, 128:208], [[0, 10], [16, 8]], OP.is_ge, 0.0, 15, -1, ["cT1"], ["cRC"])
+    eqs(CB, 1104, [[-1, 8], [-8, 16]], 0, "cPR")
+    iota(CF[0:9, 768:896], [[0, 8], [-1, 16]], 0, [], ["cM0"], 128)
+    aff(CF[0:9, 896:1024], CF[0:9, 768:896], [[0, 128]], OP.is_equal, 0.0, -8, 1, ["cM0"], ["cM1"])
+    eqs(T.SELL, 0, [[-1, 16], [-16, 8], [0, 16]], 0, "SELL")
+
+    I16, IB = CH[:, 0:128], CB[:, 0:128]
+    CP(T.SU[:, :], T.ST[:, :], ["ST"], ["SU"], 64)
+    CP(CH[:, 128:256], CB[:, 128:256], ["cPM"], ["hPM"], 64)
+    CP(CH[:, 0:128], IB, ["cI"], ["hI"], 64)
+    fill(CB[:, 512:520], 0.0, [], ["cP1a"], 64)
+    fill(CB[:, 760:768], 0.0, [], ["cP2a"], 64)
+    TTo(CB[:, 768:896], IB, CT[:, 208:336], OP.mult, ["cI", "cHi"], ["cP3"], 256)
+    TTo(CB[:, 384:512], IB, CB[:, 768:896], OP.subtract, ["cI", "cP3"], ["cP0"], 256)
+    CP(CB[:, 520:640], CB[:, 384:504], ["cP0"], ["cP1"], 64)
+    CP(CB[:, 640:760], CB[:, 776:896], ["cP3"], ["cP2"], 64)
+    CP(CH[:, 384:896], CB[:, 384:896], ["cP0", "cP1", "cP1a", "cP2", "cP2a", "cP3"], ["hP4"], 256)
+    CP(CH[:, 256:384], CB[:, 256:384], ["cA1", "cB1"], ["hF1"], 64)
+    FK, EK = ["cF0", "cF1", "cF2"], ["cE0", "cE1", "cE2"]
+    TS(CW[:, 0:384], CF[:, 0:384], 4.0, OP.mult, FK, ["wP"], 192)
+    TS(CW[:, 384:768], CF[:, 0:384], 2.0, OP.mult, FK, ["wQ"], 192)
+    TS(CW[:, 768:1152], CF[:, 384:768], 592.0, OP.mult, EK, ["wV"], 192)
+    CP(CW[:, 1152:1280], CF[:, 384:512], EK, ["wE"], 64)
+    for a in (0, 1, 2, 3, 6, 7, 8, 10, 11):
+        CP(T.NT[:, a * 256:a * 256 + 256], T.ON[0:9, 0:256], ["ON"], ["NT%d" % a], 128)
+    TS(T.CBIG[:, :], CB[:, 128:384], BIG, OP.mult, ["cPM", "cA1", "cB1"], ["CBIG"], 128)
+    TS(T.S8[:, :], CB[:, 896:1024:16], 8192.0, OP.mult, ["cEB"], ["S8"], 64)
+    TS(T.NEGI[:, :], IB, -1.0, OP.mult, ["cI"], ["NEGI"], 64)
+    QE, QO = ["QR%d" % k for k in range(0, 16, 2)], ["QR%d" % k for k in range(1, 16, 2)]
+    for k in list(range(0, 16, 2)) + list(range(1, 16, 2)):
+        if k % 4 < 2:
+            CP(T.QR[:, k::16], T.Q[:, :], ["Q"], ["QR%d" % k], 128)
+        else:
+            S(T.QR[:, k::16], T.Q[:, :], FN.Copy, ["Q"], ["QR%d" % k], 256)
+    QA = QE + QO
+    CP(T.VH[:, :], T.VS[:, :], ["VS"], ["VH"], 1024)
+
+    def late_constants():
+        CP(CH[:, 1104:1232], CB[:, 1104:1232], ["cPR"], ["hPR"], 64)
+        TTo(CW[:, 1280:1408], CF[:, 384:512], CF[:, 896:1024], OP.add, EK + ["cM1"], ["wM"], 256)
+        TS(T.MT0[:, :], T.MT0[:, :], 1.0, OP.min, ["MT0"], ["MT0"], 64)
+        CP(T.THF[:, :], T.TH[:, :], ["TH"], ["THF"], 64)
+        fill(T.VV[:, 0:16], 0.0, [], ["VV0"], 64)
+        fill(T.VV[:, 160:176], 0.0, [], ["VV10"], 64)
+        fill(T.CS[:, 128:132], 0.0, [], ["CSz"], 64)
+        x = 0
+        for L in range(3, 11):
+            for i in range(max(1, L - 5), min(5, L - 1) + 1):
+                fill(T.WT[:, x:x + 16], float(25 - (i - 1) * 5 - (L - i - 1)), [], ["WT%d" % x], 64)
+                x += 16
+
+    n = len(T.cores)
+    r = T.rank_of(core)
+    its = items(r, T, topo)
+
+    def send(k):
+        buf, c0, c1, land, asem, dst, rel = its[k]
+
+        def fn():
+            if rel is None:
+                remote(g, T, topo, core, dst, T[land][:, c0:c1], T[buf][:, c0:c1], asem, "lo%d" % k)
+            else:
+                remote(g, T, topo, core, rel, T[land][:, c0:c1], T[buf][:, c0:c1], "ri%d" % k, "lo%d" % k)
+        op("g", fn, [buf], [], 0.5, "r", "lo%d" % k, len(topo.engines(core, dst if rel is None else rel)))
+
+    def arrive(land, asem, giver, lat, after):
+        tot = 0
+        for it in items(giver, T, topo):
+            if it[4] == asem:
+                tot += len(topo.engines(T.cores[giver] if it[6] is None else it[6], core))
+        op(None, None, after, [land], 0.0, "x", asem, tot, lat)
+    for k in range(6):
+        send(k)
+    arrive("TP0", "aTP0", (r + 1) % n, 14.0, ["TO"])
+    arrive("TPn", "aTPn", (r + 2) % n, 25.0, ["TO"])
+
+    NB = T.NB[:, 0:1024]
+
+    def nt(c, a):
+        return 0 if a == 0 else (a if c == 0 else 5 + a)
+
+    def NTs(s, rows=9):
+        return T.NT[0:rows, s * 256:s * 256 + 256]
+
+    def start(t):
+        P = "PT%d" % t
+        vl = T.SU[:, t * 16:t * 16 + 16]
+        V(lambda e: e.tensor_copy(T.X0B[:, :], T.XI[:, 0:1024].indirect(vl)), ["XI0", "XI1", "XI2", "XI3", "SU"], ["X0B"], 384)
+        X = PS["xA"]
+        MM(X[0:8, 0:256], CH[:, 128:136], T.X0B[:, :], True, True, ["hPM", "X0B"], ["#xA"], 8, 256)
+        for b in (0, 1):
+            MM(X[:, 256 + b * 8:264 + b * 8], T.X0B[:, b * 128:b * 128 + 128], CH[:, 128:136], True, True, ["hPM", "X0B"], ["#xA"], 128, 8)
+        CP(T.NT[0:8, 0:256], X[0:8, 0:256], ["#xA"], ["NT0"], 256)
+        for b in (0, 1):
+            CP(T[P][:, 80 + b:96:2], X[:, 256 + b * 8:264 + b * 8], ["#xA"], [P + "s5"], 64)
+        V(lambda e: e.tensor_copy(T.NN0[:, :], NB.indirect(vl)), ["NB", "SU"], ["NN0"], 384)
+
+    def step(t, c, a, tab, tkey):
+        C = str(c)
+        P = "PT%d" % t
+        bon[0] = LEAD * (1 - c)
+        kb, wb, xb, db = ("kA", "wA", "xA", "dA") if c == 0 else ("kB", "wB", "xB", "dB")
+        K, W, X, D = PS[kb], PS[wb], PS[xb], PS[db]
+        KB, WB, XB, DB = "#" + kb, "#" + wb, "#" + xb, "#" + db
+        nn, nnk = (T.NN0, "NN0") if a == 0 else (T["NN" + C], "NN" + C)
+
+        def sl(i):
+            return 5 + i if c == 0 else 5 - i
+        if a == 0:
+            w = 128
+            p0 = 384 + 256 * c
+            MM(X[:, 0:128], CH[:, p0:p0 + 128], nn[:, 0::2], True, False, ["hP4", nnk], [XB], 128, 128)
+            MM(X[:, 0:128], CH[:, p0 + 128:p0 + 256], nn[:, 1::2], False, True, ["hP4", nnk], [XB], 128, 128)
+            E, O = T.NT[:, 0:256:2], T.NT[:, 1:256:2]
+            MM(W[:, 0:128], CW[:, 128:256], E, True, False, ["wP", "NT0"], [WB], 128, 128)
+            MM(W[:, 0:128], CW[:, 256:384], O, False, True, ["wP", "NT0"], [WB], 128, 128)
+            for z, (q0, src) in enumerate(((512, E), (640, O), (896, E), (1024, O))):
+                MM(W[:, 256:384], CW[:, q0:q0 + 128], src, z == 0, z == 3, ["wQ", "wV", "NT0"], [WB], 128, 128)
+            S(T["NPK" + C][:, :], X[:, 0:128], FN.Copy, [XB], ["NPK" + C], 128)
+            src, sk = T["NPK" + C][:, :], "NPK" + C
+            parts = ((1024, 512, "s"), (1536, 512, "s"), (0, 512, "v"), (512, 512, "v"))
+        else:
+            w = 256
+            V(lambda e: e.tensor_copy(nn[:, :], NB.indirect(T["VL" + C][:, 0:16])), ["NB", "VL" + C], [nnk], 384)
+            s0, s1 = nt(c, a - 1), nt(c, a)
+            MM(W[:, 0:256], CW[:, 0:128], NTs(s0), True, True, ["wP", "NT%d" % s0], [WB], 128, 256)
+            MM(W[:, 256:512], CW[:, 384:512], NTs(s0), True, False, ["wQ", "NT%d" % s0], [WB], 128, 256)
+            MM(W[:, 256:512], CW[0:8, 768:896], NTs(s1, 8), False, True, ["wV", "NT%d" % s1], [WB], 128, 256)
+            src, sk = nn[:, :], nnk
+            parts = ((2048, 512, "s"), (2560, 512, "s"), (3072, 512, "s"), (3584, 512, "s"), (0, 1024, "v"), (1024, 1024, "v"))
+        TTo(T["M" + C][:, 0:w], src, W[:, 0:w], OP.mult, [sk, WB], ["M" + C], w)
+        TTo(T["T" + C][:, 0:w], T["M" + C][:, 0:w], W[:, 256:256 + w], OP.add, ["M" + C, WB], ["T" + C], w)
+        TS(T["B" + C][:, 0:w], T["T" + C][:, 0:w], 4, OP.arith_shift_right, ["T" + C], ["B" + C], w, 2047, OP.bitwise_and)
+        CP(T["OF" + C][:, 0:w], T["B" + C][:, 0:w], ["B" + C], ["OF" + C], w)
+        win = tab[:, 0:2048]
+        dv, ab, xg = T["DV" + C], T["AB" + C], T["XG" + C]
+
+        def keys(nm, p, ln):
+            return ["%s%s.%d" % (nm, C, z) for z in range(p // 512, (p + ln) // 512)]
+
+        def qv(p, ln):
+            return T.QR[:, 2 * p:2 * p + 2 * ln:2] if a == 0 else T.QR[:, p:p + ln]
+        QK = QE if a == 0 else QA
+        for p, ln, e in parts:
+            off = T["OF" + C][:, p // 16:(p + ln) // 16]
+            if e == "v":
+                V(lambda en, p=p, ln=ln, off=off: en.tensor_tensor(dv[:, p:p + ln], win.indirect(off), qv(p, ln), OP.subtract),
+                  ["OF" + C, tkey] + QK, keys("dv", p, ln), ln * 1.5)
+            else:
+                op("s", lambda p=p, ln=ln, off=off: g.scalar.activation(xg[:, p % 2048:p % 2048 + ln], win.indirect(off), FN.Copy),
+                   ["OF" + C, tkey], keys("XG", p % 2048, ln), ln * 1.5 * CY + 0.07)
+        MM(K[:, 0:256], T.ON[0:33, 0:128], T.CR[:, 256 * (a == 0):256 * (a == 0) + 256], True, False, ["ON", "CR"], [KB], 128, 256)
+        pc, pw, bc = (256 + 64 * c, 64, 128 + 64 * c) if a == 0 else (128, 128, 0)
+        for b in (0, 1):
+            MM(K[:, b * 128:b * 128 + pw], nn[:, b * 128:b * 128 + 128], CH[:, pc:pc + pw], False, False, [nnk, "hPM", "hF1"], [KB], 128, pw)
+        for p, ln, e in parts:
+            if e == "v":
+                S(ab[:, p:p + ln], dv[:, p:p + ln], FN.Abs, keys("dv", p, ln), keys("ab", p, ln), ln)
+            else:
+                MM(D[:, :], IB, xg[:, p % 2048:p % 2048 + 512], True, False, ["cI"] + keys("XG", p % 2048, 512), [DB], 128, 512)
+                MM(D[:, :], T.NEGI[:, :], qv(p, 512), False, True, ["NEGI"] + QK, [DB], 128, 512)
+                S(ab[:, p:p + 512], D[:, :], FN.Abs, [DB], keys("ab", p, 512), 512)
+
+        def score(b, last):
+            stp = 8 if a == 0 else 16
+            base = b * 128 * stp
+            for k in range(stp):
+                col = b * 128 + (k * 8 if a == 0 else (k % 8) * 16 + (k // 8) * 8)
+                MM(K[:, col:col + 8], ab[:, base + k:base + 128 * stp:stp], T.S8[:, :], False, last and k == stp - 1,
+                   keys("ab", base, 128 * stp) + ["S8"], [KB], 128, 8)
+        score(0, False)
+        BQ = T["BQ" + C]
+        for j in range(a + 1):
+            s = nt(c, j)
+            x0, j0 = (j % 2) * 256, j * 256
+            MM(X[:, x0:x0 + 256], CW[0:8, 1152:1280], NTs(s, 8), True, True, ["wE", "NT%d" % s], [XB], 128, 256)
+            bk = "BQ%s%d" % (C, j)
+            TTo(BQ[:, j0:j0 + 256], nn[:, :], X[:, x0:x0 + 256], OP.is_equal, [nnk, XB], [bk], 256)
+            for b in (0, 1):
+                MM(K[:, b * 128:b * 128 + pw], BQ[:, j0 + b * 128:j0 + b * 128 + 128], T.CBIG[:, bc:bc + pw], False, False, [bk, "CBIG"], [KB], 128, pw)
+        score(1, True)
+        KD = T["KD" + C]
+        TS(KD[:, 0:16], T[P][:, sl(a) * 16:sl(a) * 16 + 16], REST, OP.add, [P + "s%d" % sl(a)], ["KR" + C], 64)
+        h = 32 if a == 0 else 64
+        SBt, L1, L2, Kt, Rt, SHt = T["SB" + C], T["L1" + C], T["L2" + C], T["K" + C], T["R" + C], T["SH" + C]
+        for b in (0, 1):
+            S(SBt[:, b * 64:b * 64 + h], K[:, b * 128 + h:b * 128 + 2 * h], FN.Copy, [KB], ["SB%s%d" % (C, b)], h)
+        for b in (0, 1):
+            TTo(L1[:, b:2 * h:2], K[:, b * 128:b * 128 + h], SBt[:, b * 64:b * 64 + h], OP.min, [KB, "SB%s%d" % (C, b)], ["L1%s%d" % (C, b)], h)
+        TTo(L2[:, 0:h], L1[:, 0:h], L1[:, h:2 * h], OP.min, ["L1%s0" % C, "L1%s1" % C], ["L2" + C], 2 * h)
+        TTo(Kt[:, 0:h // 2], L2[:, 0:h // 2], L2[:, h // 2:h], OP.min, ["L2" + C], ["K" + C], h)
+        TTo(Kt[:, 0:16], Kt[:, 0:16], KD[:, 0:16], OP.min, ["K" + C, "KR" + C], ["K" + C], 64)
+        ns = sl(a + 1)
+        out, ok = T[P][:, ns * 16:ns * 16 + 16], P + "s%d" % ns
+        if a == 0:
+            TS(Rt[:, 0:16], Kt[:, 0:16], 1023, OP.bitwise_and, ["K" + C], ["R" + C], 64)
+            CP(out, Rt[:, 0:16], ["R" + C], [ok], 64)
+        else:
+            TS(SHt[:, :], Kt[:, :], 13, OP.arith_shift_right, ["K" + C], ["SH" + C], 64)
+            TS(Rt[:, :], Kt[:, :], 1023, OP.bitwise_and, ["K" + C], ["R" + C], 64)
+            TTo(KD[:, 16:32], SHt[:, 0:16], SHt[:, 16:32], OP.is_gt, ["SH" + C], ["SL" + C], 64)
+            TTo(KD[:, 32:48], Rt[:, 16:32], Rt[:, 0:16], OP.subtract, ["R" + C], ["DF" + C], 64)
+            TTo(KD[:, 48:64], KD[:, 32:48], KD[:, 16:32], OP.mult, ["DF" + C, "SL" + C], ["D2" + C], 64)
+            TTo(out, Rt[:, 0:16], KD[:, 48:64], OP.add, ["R" + C, "D2" + C], [ok], 64)
+        if a < 4:
+            s = nt(c, a + 1)
+            for b in (0, 1):
+                MM(X[0:8, b * 128:b * 128 + 128], T[P][:, ns * 16 + b:ns * 16 + 16:2], I16, True, True, [ok, "hI"], [XB], 8, 128)
+            CP(NTs(s, 8), X[0:8, 0:256], [XB], ["NT%d" % s], 256)
+            for i in range(16):
+                MM(X[:, 256:272], T.VH[:, i * 128:i * 128 + 128], T.NT[0:8, s * 256 + i:s * 256 + 256:16], i == 0, i == 15, ["VH", "NT%d" % s], [XB], 128, 16)
+            CP(T["VL" + C][:, :], X[:, 256:272], [XB], ["VL" + C], 64)
+        bon[0] = 0.0
+
+    def lesser(el, tab, tk):
+        TS(T.TMP[:, :], tab[:, 0:2048], 0.75, OP.mult, [tk], ["TMP"], 1024, 1024.375, OP.add)
+        TS(T[el][:, :], T.TMP[:, :], -1024.0, OP.add, ["TMP"], [el], 1024)
+
+    def lessen(tab, tk, mk, el, out, okey, banks):
+        for qd in range(4):
+            b = banks[qd % len(banks)]
+            B = PS[b]
+            MM(B[:, :], IB, tab[:, qd * 512:qd * 512 + 512], True, False, ["cI", tk], ["#" + b], 128, 512)
+            for z in range(4):
+                tt = (qd * 4 + z) * 128
+                MM(B[:, z * 128:z * 128 + 128], T.SELL[:, tt:tt + 128], T[mk][:, :], False, z == 3, ["SELL", mk], ["#" + b], 128, 128)
+            TTo(out[:, qd * 512:qd * 512 + 512], B[:, :], T[el][:, qd * 512:qd * 512 + 512], OP.max, ["#" + b, el], ["%s%d" % (okey, qd)], 512)
+
+    def hot(c0, c1, kz, hk):
+        TS(T.WW[:, c0:c1], T.HH[:, c0:c1], 127, OP.bitwise_and, hk, ["WW" + kz], c1 - c0)
+        TS(T.WS[:, c0:c1], T.WW[:, c0:c1], -128.0, OP.add, ["WW" + kz], ["WS" + kz], c1 - c0)
+        for col in sorted(range(c0, c1), key=lambda z: (z % 16, z)):
+            TS(T.OH[:, col * 128:col * 128 + 128], T.I128[:, :], T.WS[:, col:col + 1], OP.is_equal, ["I128", "WS" + kz], ["OH%d" % col], 64)
+
+    def rings(t, tab, tk):
+        P = "PT%d" % t
+        pt, JS = T[P], T.JS
+        pk = [P + "s%d" % i for i in range(11)]
+        uk, hw = [P + "u%d" % i for i in range(3)], ["HHe", "HHx", "HHy"]
+        for z, (c0, c1, kk) in enumerate(((16, 160, pk[1:10]), (0, 16, pk[0:1]), (160, 176, pk[10:11]))):
+            TS(T.U[:, c0:c1], pt[:, c0:c1], 2.0, OP.mult, kk, [uk[z]], c1 - c0, 1.0, OP.add)
+        for z, (c0, c1, kk, ku) in enumerate(((16, 128, pk[1:10], uk[0:1]), (0, 16, pk[0:3], uk[0:2]), (128, 144, pk[8:11], [uk[0], uk[2]]))):
+            TTo(T.PR[:, c0:c1], T.U[:, c0:c1], T.U[:, c0 + 32:c1 + 32], OP.mult, ku, ["PR%d" % z], 2 * (c1 - c0))
+            TS(T.V5[:, c0:c1], pt[:, c0 + 16:c1 + 16], 592.0, OP.mult, kk, ["V5%d" % z], c1 - c0)
+            TTo(T.TT[:, c0:c1], T.PR[:, c0:c1], T.V5[:, c0:c1], OP.add, ["PR%d" % z, "V5%d" % z], ["TT%d" % z], 2 * (c1 - c0))
+            TS(T.HH[:, c0:c1], T.TT[:, c0:c1], 4, OP.arith_shift_right, ["TT%d" % z], [hw[z]], c1 - c0, 2047, OP.bitwise_and)
+        hot(16, 128, "e", ["HHe"])
+        x = 0
+        ek = []
+        for L in range(3, 11):
+            i0 = max(1, L - 5)
+            m = (min(5, L - 1) - i0 + 1) * 16
+            a0, b0 = (5 + i0) * 16, (5 + i0 - L) * 16
+            TTo(T.EQ[:, x:x + m], pt[:, a0:a0 + m], pt[:, b0:b0 + m], OP.is_equal, pk, ["EQ%d" % L], 2 * m)
+            ek.append("EQ%d" % L)
+            x += m
+        TTo(T.EW[:, :], T.EQ[:, :], T.WT[:, :], OP.mult, ek + ["WT%d" % z for z in range(0, 384, 16)], ["EW"], 768)
+        TTo(T.E1[:, :], T.EW[:, 0:192], T.EW[:, 192:384], OP.max, ["EW"], ["E1"], 384)
+        TTo(T.E2[:, :], T.E1[:, 0:96], T.E1[:, 96:192], OP.max, ["E1"], ["E2"], 192)
+        TTo(T.E3[:, 0:48], T.E2[:, 0:48], T.E2[:, 48:96], OP.max, ["E2"], ["E3"], 96)
+        TTo(T.E3[:, 48:64], T.E3[:, 0:16], T.E3[:, 16:32], OP.max, ["E3"], ["E4"], 64)
+        JW, JF, JI, JU, JL, JJ, VJ, PJ = [JS[:, z * 16:z * 16 + 16] for z in range(8)]
+        TTo(JW, T.E3[:, 48:64], T.E3[:, 32:48], OP.max, ["E3", "E4"], ["JW"], 64)
+        TS(JF, JW, 0.5, OP.is_ge, ["JW"], ["JF"], 64)
+        TS(T.JR[:, :], JW, -0.2, OP.mult, ["JW"], ["JR"], 64, 5.6, OP.add)
+        TTo(JI, T.JR[:, :], JF, OP.mult, ["JR", "JF"], ["JI"], 64)
+        TS(JU, T.JR[:, :], -4.0, OP.mult, ["JR"], ["JU"], 64, 31.0, OP.add)
+        TTo(JL, JU, JW, OP.subtract, ["JU", "JW"], ["JL"], 64)
+        TTo(T.IL[:, 16:32], JL, JF, OP.mult, ["JL", "JF"], ["ILl"], 64)
+        TTo(JJ, T.IL[:, 16:32], JI, OP.subtract, ["ILl", "JI"], ["JJ"], 64)
+        for m in range(0, 5):
+            z = (5 + m) * 16
+            TS(T.VV[:, z:z + 16], JI, m + 0.5, OP.is_ge, ["JI"], ["VV%d" % (5 + m)], 64)
+            if m:
+                z = (5 - m) * 16
+                TS(T.VV[:, z:z + 16], JJ, m + 0.5, OP.is_ge, ["JJ"], ["VV%d" % (5 - m)], 64)
+        vk = ["VV%d" % i for i in range(11)]
+        MI, MJ = T.MI[:, 0:80], T.MI[:, 80:160]
+        TTo(MI, T.VV[:, 80:160], T.VV[:, 96:176], OP.subtract, vk, ["MI"], 160)
+        TTo(MJ, T.VV[:, 16:96], T.VV[:, 0:80], OP.subtract, vk, ["MJ"], 160)
+        TTo(T.JP[:, 0:80], MI, pt[:, 80:160], OP.mult, ["MI"] + pk, ["JP0"], 160)
+        TTo(T.JP[:, 80:160], MI, pt[:, 96:176], OP.mult, ["MI"] + pk, ["JP1"], 160)
+        TTo(T.JP[:, 160:240], MJ, pt[:, 16:96], OP.mult, ["MJ"] + pk, ["JP2"], 160)
+        J = PS["kA"]
+        for z in range(3):
+            for k in range(5):
+                MM(J[:, z * 16:z * 16 + 16], I16, T.JP[:, z * 80 + k * 16:z * 80 + k * 16 + 16], k == 0, k == 4, ["hI", "JP%d" % z], ["#kA"], 128, 16)
+        TS(T.UJ[:, :], J[:, 0:48], 2.0, OP.mult, ["#kA"], ["UJ"], 64, 1.0, OP.add)
+        TS(VJ, J[:, 16:32], 592.0, OP.mult, ["#kA"], ["VJ"], 64)
+        TTo(PJ, T.UJ[:, 0:16], T.UJ[:, 32:48], OP.mult, ["UJ"], ["PJ"], 64)
+        TTo(T.TT[:, 144:160], PJ, VJ, OP.add, ["PJ", "VJ"], ["TTb"], 64)
+        TS(T.HH[:, 144:160], T.TT[:, 144:160], 4, OP.arith_shift_right, ["TTb"], ["HHb"], 64, 2047, OP.bitwise_and)
+        hk = hw + ["HHb"]
+        TS(T.HS[:, :], T.HH[:, :], -2048.0, OP.add, hk, ["HS"], 160)
+        TTo(T.HV[:, 0:144], T.HS[:, 0:144], T.VV[:, 16:160], OP.mult, ["HS"] + vk, ["HVa"], 288)
+        TTo(T.HV[:, 144:160], T.HS[:, 144:160], T.VV[:, 80:96], OP.mult, ["HS"] + vk, ["HVb"], 64)
+        TS(T.TB[:, :], T.HH[:, :], 7, OP.arith_shift_right, hk, ["TB"], 160)
+        TS(T.TBP[:, :], T.TB[:, :], 2.0, OP.add, ["TB"], ["TBP"], 160)
+        TTo(T.TV[:, 0:144], T.TBP[:, 0:144], T.VV[:, 16:160], OP.mult, ["TBP"] + vk, ["TVa"], 288)
+        TTo(T.TV[:, 144:160], T.TBP[:, 144:160], T.VV[:, 80:96], OP.mult, ["TBP"] + vk, ["TVb"], 64)
+        X, X2 = PS["xA"], PS["xB"]
+        for b in (0, 1):
+            MM(X[0:80, b * 128:b * 128 + 128], T.HV[:, b::2], I16, True, True, ["HVa", "HVb", "hI"], ["#xA"], 80, 128)
+        CP(T.HT[:, :], X[0:80, 0:256], ["#xA"], ["HT"], 256)
+        MM(X2[:, 0:256], CH[0:80, 1104:1232], T.HT[:, :], True, True, ["hPR", "HT"], ["#xB"], 128, 256)
+        TS(T.OFR[:, :], X2[:, 0:256], 2048.0, OP.add, ["#xB"], ["OFR"], 256)
+        win = tab[:, 0:2064]
+        op("s", lambda: g.scalar.activation(T.XR[:, 2048:4096], win.indirect(T.OFR[:, 128:256]), FN.Copy), ["OFR", tk, tk + "z"], ["XR1"], 3072 * CY)
+        V(lambda e: e.tensor_copy(T.XR[:, 0:2048], win.indirect(T.OFR[:, 0:128])), ["OFR", tk, tk + "z"], ["XR0"], 3072)
+        for b in (0, 1):
+            MM(X[0:80, b * 128:b * 128 + 128], T.TV[:, b::2], I16, True, True, ["TVa", "TVb", "hI"], ["#xA"], 80, 128)
+        CP(T.TVL[:, :], X[0:80, 0:256], ["#xA"], ["TVL"], 256)
+        hot(0, 16, "a", hk)
+        hot(128, 160, "b", hk)
+        B, W = PS["kB"], PS["wA"]
+        for b in (0, 1):
+            for m in range(10):
+                MM(B[:, b * 128:b * 128 + 128], IB, T.XR[:, b * 2048 + m:(b + 1) * 2048:16], m == 0, m == 9, ["cI", "XR%d" % b], ["#kB"], 128, 128)
+        for b in (0, 1):
+            TS(T.CMP[:, b * 128:b * 128 + 128], B[:, b * 128:b * 128 + 128], T.THF[:, 0:1], OP.is_ge, ["#kB", "THF"], ["CMP%d" % b], 128)
+        MM(W[0:80, 0:256], CB[:, 1024:1104], T.CMP[:, :], True, True, ["CMP0", "CMP1", "cRC"], ["#wA"], 80, 256)
+        TS(T.HVY[:, :], W[0:80, 0:256], 8.5, OP.is_ge, ["#wA"], ["HVY"], 256)
+        TTo(T.TM[:, :], T.TVL[:, :], T.HVY[:, :], OP.mult, ["TVL", "HVY"], ["TM"], 512)
+        C = PS["wB"]
+        z = 0
+        for b in (0, 1):
+            for c0 in range(0, 1280, 512):
+                c1 = min(1280, c0 + 512)
+                bn = ("xA", "wA", "dA")[z % 3]
+                z += 1
+                MM(PS[bn][:, 0:c1 - c0], T.TM[:, b * 128:b * 128 + 128], T.RT[:, c0:c1], True, True, ["TM", "RT"], ["#" + bn], 128, c1 - c0)
+                TTo(T.TL[:, b * 1280 + c0:b * 1280 + c1], PS[bn][:, 0:c1 - c0], T.THR[:, 0:c1 - c0], OP.is_ge, ["#" + bn, "THR"], ["TL%d.%d" % (b, c0 // 512)], c1 - c0)
+        for gr in range(8):
+            for z, (m, b) in enumerate([(m, b) for b in (0, 1) for m in range(10)]):
+                col = m * 16 + gr * 2 + b
+                l0 = (m * 8 + gr) * 16
+                MM(C[:, gr * 16:gr * 16 + 16], T.OH[:, col * 128:col * 128 + 128], T.TL[:, b * 1280 + l0:b * 1280 + l0 + 16], z == 0, z == 19,
+                   ["OH%d" % col, "TL%d.%d" % (b, l0 // 512)], ["#wB"], 128, 16)
+        TTo(T.CS[:, 0:128], C[:, 0:128], T.MT0[:, :], OP.mult, ["#wB", "MT0"], ["CS"], 128)
+        TTo(T.DD[:, :], C[:, 0:128], T.CS[:, 1:129], OP.subtract, ["#wB", "CS", "CSz"], ["DD"], 128)
+        TS(T.MK[:, :], T.DD[:, :], 1.0, OP.min, ["DD"], ["MK"], 128, -512.0, OP.mult)
+        MM(X[:, 0:128], T.MK[:, :], IB, True, True, ["MK", "cI"], ["#xA"], 128, 128)
+        S(T.MKT[:, :], X[:, 0:128], FN.Copy, ["#xA"], ["MKT"], 128)
+
+    def show(t):
+        P = "PT%d" % t
+        pt = T[P]
+        D, E = PS["dA"], PS["dB"]
+        TTo(T.IL[:, 0:16], T.JS[:, 32:48], T.JS[:, 16:32], OP.add, ["JI", "JF"], ["ILi"], 64)
+        for b in (0, 1):
+            MM(D[0:8, b * 128:b * 128 + 128], pt[:, 160 + b:176:2], I16, True, True, [P + "s10", "hI"], ["#dA"], 8, 128)
+        for b in (0, 1):
+            MM(D[0:8, 256 + b * 128:384 + b * 128], T.IL[:, b:16:2], I16, True, True, ["ILi", "hI"], ["#dA"], 8, 128)
+        for b in (0, 1):
+            MM(E[0:8, b * 128:b * 128 + 128], T.IL[:, 16 + b:32:2], I16, True, True, ["ILl", "hI"], ["#dB"], 8, 128)
+        CP(NTs(5, 8), D[0:8, 0:256], ["#dA"], ["NT5"], 256)
+        CP(NTs(10, 8), D[0:8, 256:512], ["#dA"], ["NT10"], 256)
+        CP(NTs(11, 8), E[0:8, 0:256], ["#dB"], ["NT11"], 256)
+        for z in (0, 1):
+            MM(D[:, z * 256:z * 256 + 256], CW[:, 1280:1408], NTs(10 + z), True, True, ["wM", "NT%d" % (10 + z)], ["#dA"], 128, 256)
+        for i in range(6):
+            MM(E[:, 0:256], T.VH[:, i * 128:i * 128 + 128], NTs(i, 8), i == 0, i == 5, ["VH", "NT%d" % i], ["#dB"], 128, 256)
+        R1, R2 = D[:, 0:256], D[:, 256:512]
+        TS(T.YN[:, :], R1, 0.5, OP.is_le, ["#dA"], ["YN"], 256)
+        TS(T.YM[:, :], R1, 0.5, OP.is_ge, ["#dA"], ["YM"], 256)
+        TTo(T.YP[:, :], T.YN[:, :], R2, OP.mult, ["#dA", "YN"], ["YP"], 256)
+        TS(T.YB[:, 256:512], R2, 0.5, OP.is_le, ["#dA"], ["YB1"], 256, -1.0, OP.mult)
+        TTo(T.YB[:, 0:256], T.YM[:, :], E[:, 0:256], OP.mult, ["#dB", "YM"], ["YB0"], 256)
+        for j in range(1, 5):
+            k0 = (j - 1) * 256
+            MM(E[:, 256:512], CW[0:8, 1152:1280], NTs(5 + j, 8), True, True, ["wE", "NT%d" % (5 + j)], ["#dB"], 128, 256)
+            TS(T.YK[:, k0:k0 + 256], T.YP[:, :], float(j), OP.is_equal, ["YP"], ["YK%d" % j], 128)
+            TTo(T.YB[:, 256 + j * 256:512 + j * 256], T.YK[:, k0:k0 + 256], E[:, 256:512], OP.mult, ["YK%d" % j, "#dB"], ["YB%d" % (j + 1)], 256)
+        for z in range(6):
+            MM(D[:, 0:256], I16, T.YB[:, z * 256:z * 256 + 256], z == 0, z == 5, ["hI", "YB%d" % z], ["#dA"], 128, 256)
+        S(T.YR[:, t * 256:t * 256 + 256], D[:, 0:256], FN.Copy, ["#dA"], ["YR%d" % t], 256)
+        DMA("y", T.yr[:, t * 256:t * 256 + 256], T.YR[:, t * 256:t * 256 + 256], ["YR%d" % t], [])
+
+    start(0)
+    for a in range(5):
+        step(0, 0, a, T.TO, "TO")
+        step(0, 1, a, T.TP0, "TP0")
+    late_constants()
+    lesser("EL0", T.TO, "TO")
+    lesser("ELn", T.TPn, "TPn")
+    rings(0, T.TO, "TO")
+    send(6)
+    arrive("MKP", "aMK", (r + 2) % n, 7.0, ["MKT"])
+    show(0)
+    lessen(T.TO, "TO", "MKT", "EL0", T.TO1, "T1q", ("kA", "kB", "xB", "wA"))
+    op(None, None, ["T1q%d" % q for q in range(4)], ["TO1"], 0.0, "n")
+    start(1)
+    lessen(T.TPn, "TPn", "MKP", "ELn", T.TP1, "P1q", ("dB",))
+    op(None, None, ["P1q%d" % q for q in range(4)], ["TP1"], 0.0, "n")
+    for a in range(5):
+        step(1, 0, a, T.TO1, "TO1")
+        step(1, 1, a, T.TP1, "TP1")
+    lesser("EL1", T.TO1, "TO1")
+    rings(1, T.TO1, "TO1")
+    show(1)
+    lessen(T.TO1, "TO1", "MKT", "EL1", T.TO2, "T2q", ("kA", "kB", "xB", "wA"))
+    for qd in range(4):
+        DMA("y" if qd % 2 == 0 else "s", T.ye[:, qd * 512:qd * 512 + 512], T.TO2[:, qd * 512:qd * 512 + 512], ["T2q%d" % qd], [])
+    for o in ops:
+        more = set()
+        for d in o["deps"]:
+            if ops[d]["kind"] == "n":
+                more |= ops[d]["deps"]
+            else:
+                more.add(d)
+        o["deps"] = more
+    return ops
+
+
+def schedule(ops):
+    n = len(ops)
+    wake, same = 0.12, 0.04
+    succ = [[] for _ in range(n)]
+    need = [0] * n
+    for i, o in enumerate(ops):
+        for d in o["deps"]:
+            succ[d].append((i, False))
+            need[i] += 1
+        for d in o["order"]:
+            succ[d].append((i, True))
+            need[i] += 1
+    prio = [0.0] * n
+    for i in range(n - 1, -1, -1):
+        best = 0.0
+        for j, od in succ[i]:
+            best = max(best, prio[j] + (0.0 if od else (wake if ops[j]["q"] != ops[i]["q"] else same)))
+        prio[i] = best + ops[i]["cost"] + ops[i]["lat"]
+    prio = [prio[i] + ops[i]["bon"] for i in range(n)]
+    ready, free, order = {}, {}, []
+    tready, fin = [0.0] * n, [0.0] * n
+    for i in range(n):
+        if need[i] == 0:
+            ready.setdefault(ops[i]["q"], []).append(i)
+    while len(order) < n:
+        bq, bt = None, 1e18
+        for q in ready:
+            for i in ready[q]:
+                s = max(free.get(q, 0.0), tready[i])
+                if s < bt:
+                    bt, bq = s, q
+        lst = ready[bq]
+        pick, pp = None, -1.0
+        for i in lst:
+            if max(free.get(bq, 0.0), tready[i]) <= bt + 0.1 and prio[i] > pp:
+                pick, pp = i, prio[i]
+        lst.remove(pick)
+        if not lst:
+            del ready[bq]
+        o = ops[pick]
+        s = max(free.get(bq, 0.0), tready[pick])
+        if bq is not None:
+            free[bq] = s + o["cost"]
+        fin[pick] = s + o["cost"] + o["lat"]
+        order.append(pick)
+        for j, od in succ[pick]:
+            tj = s if od else fin[pick] + (wake if ops[j]["q"] != o["q"] else same)
+            tready[j] = max(tready[j], tj)
+            need[j] -= 1
+            if need[j] == 0:
+                ready.setdefault(ops[j]["q"], []).append(j)
+    return order
+
+
+def emit(g, T, ops, order):
+    eng = {"v": g.vector, "s": g.scalar, "t": g.tensor, "g": g, "y": g.sync}
+    csem = {"v": "v", "s": "s", "t": "t", "g": "gc"}
+    count, final = {}, {}
+    know = {q: {} for q in eng}
+    mark = [None] * len(ops)
+    after = [None] * len(ops)
+    for i in order:
+        o = ops[i]
+        q = o["q"]
+        if o["kind"] == "n":
+            continue
+        if o["kind"] == "x":
+            mark[i] = (o["sem"], o["val"])
+            after[i] = {o["sem"]: o["val"]}
+            final[o["sem"]] = o["val"]
+            continue
+        K = know[q]
+        for d in sorted(o["deps"], key=lambda d: -sum(after[d].values())):
+            s, v = mark[d]
+            if K.get(s, 0) >= v:
+                continue
+            eng[q].wait_ge(T.sem[s], v)
+            for s2, v2 in after[d].items():
+                if K.get(s2, 0) < v2:
+                    K[s2] = v2
+        if q == "g" and o["kind"] == "c" and K.get("gc", 0) < count.get("gc", 0):
+            g.wait_ge(T.sem["gc"], count["gc"])
+            K["gc"] = count["gc"]
+        ins = o["fn"]()
+        if o["kind"] == "c":
+            s = csem[q]
+            count[s] = count.get(s, 0) + 1
+            ins.then_inc(T.sem[s], 1)
+            mark[i] = (s, count[s])
+        elif o["kind"] == "d":
+            ins.then_inc(T.sem[o["sem"]], 16)
+            mark[i] = (o["sem"], 16)
+        else:
+            mark[i] = (o["sem"], o["val"])
+        final[mark[i][0]] = mark[i][1]
+        after[i] = dict(K)
+        after[i][mark[i][0]] = mark[i][1]
+    for s in final:
+        if know["g"].get(s, 0) < final[s]:
+            g.wait_ge(T.sem[s], final[s])
+
+
+def rank_program(g, core, T, topo):
+    if T.rank_of(core) is None:
+        hand_on(g, core, T, topo)
+        return
+    ops = build(g, core, T, topo)
+    if "order" not in ORDERS:
+        ORDERS["order"] = schedule(ops)
+    emit(g, T, ops, ORDERS["order"])

@@ -11,24 +11,24 @@ for _n, _p, _w, _t in (
         ("NB", 128, 1024, I32), ("XI", 128, 1024, I32), ("TO", 128, 2064, B16), ("TO1", 128, 2064, B16), ("TO2", 128, 2048, B16),
         ("TP0", 128, 2048, B16), ("TPn", 128, 2048, B16), ("TP1", 128, 2048, B16), ("EL0", 128, 2048, B16), ("ELn", 128, 2048, B16),
         ("EL1", 128, 2048, B16), ("TMP", 128, 2048, H16), ("ST", 128, 32, I32), ("SU", 128, 32, "uint16"), ("TH", 128, 1, I32),
-        ("THF", 128, 1, F32), ("Q", 128, 256, B16), ("QR", 128, 4096, B16), ("ON", 128, 2048, B16), ("CB", 128, 1232, B16),
-        ("CT", 128, 336, B16), ("CH", 128, 1232, H16), ("CF", 9, 1024, B16), ("CW", 9, 1408, H16), ("VS", 8, 2048, B16),
-        ("VH", 8, 2048, H16), ("SELL", 128, 2048, B16), ("CBIG", 128, 256, B16), ("S8", 128, 8, B16), ("NEGI", 128, 128, B16),
-        ("CR", 33, 512, B16), ("I128", 128, 128, B16), ("THR", 128, 512, B16), ("RT", 80, 1280, B16), ("MT0", 128, 128, B16),
+        ("THF", 128, 1, F32), ("Q", 128, 256, B16), ("QR", 128, 4096, B16), ("ON", 128, 2048, B16), ("CB", 128, 2384, B16),
+        ("CT", 128, 464, B16), ("CH", 128, 2512, H16), ("C2", 128, 512, H16), ("CF", 9, 1024, B16), ("CW", 9, 1408, H16),
+        ("VS", 8, 2048, B16), ("VH", 8, 2048, H16), ("SELL", 128, 2048, B16), ("CBIG", 128, 256, B16), ("S8", 128, 8, B16),
+        ("NEGI", 128, 128, B16), ("CR", 33, 512, B16), ("I128", 128, 128, B16), ("RT", 97, 1280, B16), ("MT0", 128, 128, B16),
         ("WT", 128, 384, B16), ("NT", 9, 3072, H16), ("X0B", 128, 256, H16), ("PT0", 128, 176, H16), ("PT1", 128, 176, H16),
         ("NPK0", 128, 128, F32), ("NPK1", 128, 128, F32), ("U", 128, 176, F32), ("PR", 128, 144, F32), ("V5", 128, 144, F32),
         ("TT", 128, 160, I32), ("HH", 128, 160, I32), ("EQ", 128, 384, B16), ("EW", 128, 384, B16), ("E1", 128, 192, B16),
         ("E2", 128, 96, B16), ("E3", 128, 64, B16), ("JS", 128, 128, F32), ("JR", 128, 16, I32), ("IL", 128, 32, H16),
         ("VV", 128, 176, F32), ("MI", 128, 160, F32), ("JP", 128, 240, H16), ("UJ", 128, 48, F32), ("WW", 128, 160, I32),
         ("TB", 128, 160, I32), ("TBP", 128, 160, F32), ("TV", 128, 160, H16), ("TVL", 80, 256, B16), ("HS", 128, 160, F32),
-        ("HV", 128, 160, H16), ("WS", 128, 160, F32), ("HT", 80, 256, H16), ("OFR", 128, 256, "uint16"), ("XR", 128, 4096, B16),
-        ("CMP", 128, 256, B16), ("HVY", 80, 256, B16), ("TM", 80, 256, B16), ("OH", 128, 20480, B16), ("TL", 128, 2560, B16),
+        ("HV", 128, 160, H16), ("WS", 128, 320, F32), ("HT", 80, 256, H16), ("OFR", 128, 256, "uint16"), ("XR", 128, 2560, B16),
+        ("CMP", 128, 256, B16), ("HVY", 80, 256, B16), ("TM", 97, 256, B16), ("OH", 128, 20480, B16), ("TL", 128, 2560, B16),
         ("CS", 128, 132, F32), ("DD", 128, 128, F32), ("MK", 128, 128, B16), ("MKT", 128, 128, B16), ("MKP", 128, 128, B16),
         ("YN", 128, 256, H16), ("YM", 128, 256, H16), ("YP", 128, 256, H16), ("YK", 128, 1024, H16), ("YB", 128, 1536, H16),
         ("YR", 128, 512, F32)):
     SCRATCH[_n] = ("sbuf", [_p, _w], _t)
 for _c in "01":
-    for _n, _w, _t in (("NN", 256, H16), ("M", 256, F32), ("T", 256, I32), ("B", 256, I32), ("OF", 256, "uint16"), ("DV", 2048, B16),
+    for _n, _w, _t in (("NN", 256, H16), ("M", 256, F32), ("T", 256, I32), ("B", 256, I32), ("OF", 256, "uint16"), ("DV", 2560, B16),
                        ("AB", 4096, B16), ("XG", 2048, B16), ("BQ", 1280, B16), ("SB", 128, F32), ("L1", 128, F32), ("L2", 64, F32),
                        ("K", 32, I32), ("KD", 64, F32), ("SH", 32, I32), ("R", 32, I32), ("VL", 16, "uint16")):
         SCRATCH[_n + _c] = ("sbuf", [128, _w], _t)
@@ -43,6 +43,11 @@ SEMAPHORES += ["ri%d" % i for i in range(NITEM)] + ["lo%d" % i for i in range(NI
 CY = 0.00104
 TCY = 0.00075
 LEAD = 6.0
+SHOT = (1, 2, 3, 4)
+HINT = {"vM1": -2.0, "vOF0": -5.0, "vBQ1": 1.0, "vNN0": -0.5, "t#kA": -0.5, "t#xB": 0.5, "sab0": -28.5, "vCSz": 13.0, "vYP": -8.0,
+        "vOH": -7.0, "vhF": -20.0, "vWWe": -3.5, "vVL0": -2.5, "vMJ": -2.5, "vTVb": -2.0, "sXG0": -8.5, "vwP": -4.0, "sXG1": -0.5,
+        "vMK": 7.0, "vcPa": 2.0, "vSH1": 16.0, "vWSb": -5.0, "vcE": 10.5, "vhPS": -6.0, "vD20": 1.0, "vPTu": -4.0, "vWWa": 1.5,
+        "vNT": 1.5, "t#dA": 0.5, "vTHF": -0.5, "vJR": 1.0, "vJP": -2.0, "vTMz": 8.5, "vR1": 5.0, "vDD": 0.5}
 ORDERS = {}
 
 
@@ -94,6 +99,15 @@ def build(g, core, T, topo):
     lastw, reads, bank = {}, {}, {}
     bon = [0.0]
 
+    def hint(q, W):
+        if not W or q is None:
+            return 0.0
+        w = W[0].split(".")[0]
+        for name in (w, w[:3], "".join(c for c in w if not c.isdigit())):
+            if q + name in HINT:
+                return HINT[q + name]
+        return 0.0
+
     def op(q, fn, R, W, cost, kind="c", sem=None, val=1, lat=0.0):
         n = len(ops)
         deps, order = set(), set()
@@ -121,7 +135,7 @@ def build(g, core, T, topo):
                 reads[k] = []
         deps.discard(n)
         order.discard(n)
-        ops.append(dict(q=q, fn=fn, deps=deps, order=(order - deps if q == "t" else set()), cost=cost, lat=lat, kind=kind, sem=sem, val=val, bon=bon[0]))
+        ops.append(dict(q=q, fn=fn, deps=deps, order=(order - deps if q == "t" else set()), cost=cost, lat=lat, kind=kind, sem=sem, val=val, bon=bon[0] + hint(q, W)))
 
     def V(fn, R, W, n):
         op("v", lambda: fn(g.vector), R, W, max(64, n) * CY + 0.03)
@@ -141,8 +155,8 @@ def build(g, core, T, topo):
     def fill(ap, c, R, W, n):
         V(lambda e: e.memset(ap, c), R, W, n)
 
-    def S(out, a, f, R, W, n):
-        op("s", lambda: g.scalar.activation(out, a, f), R, W, max(64, n) * CY + 0.05)
+    def S(out, a, f, R, W, n, **kw):
+        op("s", lambda: g.scalar.activation(out, a, f, **kw), R, W, max(64, n) * CY + 0.05)
 
     def MM(out, l, r, st, sp, R, W, m, n):
         op("t", lambda: g.tensor.matmul(out, l, r, st, sp), R, W, max(min(64, m), n) * TCY + 0.01)
@@ -209,14 +223,18 @@ def build(g, core, T, topo):
     aff(CB[:, 896:1024], CT[:, 0:128], [[16, 8], [0, 16]], OP.is_ge, 0.0, 15, -1, ["cT0"], ["cEB"])
     eqs(T.VS, 0, [[1, 16], [-16, 8], [-1, 16]], 0, "VS", 8, 16)
     iota(T.I128[:, :], [[1, 128]], -128, [], ["I128"], 128)
-    iota(T.THR[:, :], [[0, 32], [1, 16]], 2, [], ["THR"], 512)
-    eqs(T.RT, 0, [[-1, 80], [0, 16]], 0, "RT", 80)
+    eqs(T.RT, 0, [[-1, 80], [0, 16]], 0, "RT", 97)
+    iota(T.RT[96:97, :], [[0, 80], [-1, 16]], -2, ["RT"], ["RT"], 1280)
     iota(T.MT0[:, :], [[0, 8], [1, 16]], 0, [], ["MT0"], 128)
     aff(CT[:, 128:208], T.ON[:, 0:80], [[0, 10], [-16, 8]], OP.is_ge, 0.0, 0, 1, ["ON"], ["cT1"])
     aff(CB[:, 1024:1104], CT[:, 128:208], [[0, 10], [16, 8]], OP.is_ge, 0.0, 15, -1, ["cT1"], ["cRC"])
-    eqs(CB, 1104, [[-1, 8], [-8, 16]], 0, "cPR")
+    eqs(CB, 1104, [[-1, 8], [1000, 2], [-8, 8]], 0, "cPR", 80)
+    eqs(CB, 1232, [[-1, 8], [1000, 2], [-8, 8]], -1000, "cPS", 80)
+    for z in range(8):
+        eqs(CB, 1360 + z * 128, [[-1, 8], [1000, 8], [-8, 2]], -64 - 1000 * z, "cPT%d" % z, 80)
     iota(CF[0:9, 768:896], [[0, 8], [-1, 16]], 0, [], ["cM0"], 128)
     aff(CF[0:9, 896:1024], CF[0:9, 768:896], [[0, 128]], OP.is_equal, 0.0, -8, 1, ["cM0"], ["cM1"])
+    eqs(CT, 336, [[-1, 128]], -1, "cSF")
     eqs(T.SELL, 0, [[-1, 16], [-16, 8], [0, 16]], 0, "SELL")
 
     I16, IB = CH[:, 0:128], CB[:, 0:128]
@@ -251,13 +269,18 @@ def build(g, core, T, topo):
     CP(T.VH[:, :], T.VS[:, :], ["VS"], ["VH"], 1024)
 
     def late_constants():
-        CP(CH[:, 1104:1232], CB[:, 1104:1232], ["cPR"], ["hPR"], 64)
+        CP(CH[0:80, 1104:1232], CB[0:80, 1104:1232], ["cPR"], ["hPR"], 64)
+        CP(CH[0:80, 1360:2512], CB[0:80, 1232:2384], ["cPS"] + ["cPT%d" % z for z in range(8)], ["hPS"], 576)
         TTo(CW[:, 1280:1408], CF[:, 384:512], CF[:, 896:1024], OP.add, EK + ["cM1"], ["wM"], 256)
         TS(T.MT0[:, :], T.MT0[:, :], 1.0, OP.min, ["MT0"], ["MT0"], 64)
         CP(T.THF[:, :], T.TH[:, :], ["TH"], ["THF"], 64)
         fill(T.VV[:, 0:16], 0.0, [], ["VV0"], 64)
         fill(T.VV[:, 160:176], 0.0, [], ["VV10"], 64)
+        TTo(CH[:, 1232:1360], IB, CT[:, 336:464], OP.subtract, ["cI", "cSF"], ["hDM"], 256)
+        fill(T.TM[:, :], 0.0, [], ["TMz"], 64)
+        fill(T.TM[96:97, :], 1.0, ["TMz"], ["TMz"], 64)
         fill(T.CS[:, 128:132], 0.0, [], ["CSz"], 64)
+        fill(T.CS[:, 129:130], 100.0, ["CSz"], ["CSz"], 64)
         x = 0
         for L in range(3, 11):
             for i in range(max(1, L - 5), min(5, L - 1) + 1):
@@ -342,7 +365,7 @@ def build(g, core, T, topo):
             MM(W[:, 256:512], CW[:, 384:512], NTs(s0), True, False, ["wQ", "NT%d" % s0], [WB], 128, 256)
             MM(W[:, 256:512], CW[0:8, 768:896], NTs(s1, 8), False, True, ["wV", "NT%d" % s1], [WB], 128, 256)
             src, sk = nn[:, :], nnk
-            parts = ((2048, 512, "s"), (2560, 512, "s"), (3072, 512, "s"), (3584, 512, "s"), (0, 1024, "v"), (1024, 1024, "v"))
+            parts = tuple((z, 512, "s") for z in (2560, 3072, 3584)) + tuple((z, 512, "v") for z in range(0, 2560, 512))
         TTo(T["M" + C][:, 0:w], src, W[:, 0:w], OP.mult, [sk, WB], ["M" + C], w)
         TTo(T["T" + C][:, 0:w], T["M" + C][:, 0:w], W[:, 256:256 + w], OP.add, ["M" + C, WB], ["T" + C], w)
         TS(T["B" + C][:, 0:w], T["T" + C][:, 0:w], 4, OP.arith_shift_right, ["T" + C], ["B" + C], w, 2047, OP.bitwise_and)
@@ -444,8 +467,14 @@ def build(g, core, T, topo):
     def hot(c0, c1, kz, hk):
         TS(T.WW[:, c0:c1], T.HH[:, c0:c1], 127, OP.bitwise_and, hk, ["WW" + kz], c1 - c0)
         TS(T.WS[:, c0:c1], T.WW[:, c0:c1], -128.0, OP.add, ["WW" + kz], ["WS" + kz], c1 - c0)
-        for col in sorted(range(c0, c1), key=lambda z: (z % 16, z)):
-            TS(T.OH[:, col * 128:col * 128 + 128], T.I128[:, :], T.WS[:, col:col + 1], OP.is_equal, ["I128", "WS" + kz], ["OH%d" % col], 64)
+        if kz == "e":
+            S(T.WS[:, 160 + c0:160 + c1], T.WS[:, c0:c1], FN.Copy, ["WSe"], ["WB"], c1 - c0, bias=100.0, scale=200.0)
+        for col in sorted(range(c0, c1), key=lambda z: (z % 2, z % 16, z)):
+            o = T.OH[:, col * 128:col * 128 + 128]
+            if col // 16 in SHOT:
+                S(o, T.I128[:, :], FN.Sigmoid, ["I128", "WB"], ["OH%d" % col], 128, bias=T.WS[:, 160 + col:161 + col], scale=-200.0)
+            else:
+                TS(o, T.I128[:, :], T.WS[:, col:col + 1], OP.is_equal, ["I128", "WS" + kz], ["OH%d" % col], 64)
 
     def rings(t, tab, tk):
         P = "PT%d" % t
@@ -517,25 +546,34 @@ def build(g, core, T, topo):
         for b in (0, 1):
             MM(X[0:80, b * 128:b * 128 + 128], T.HV[:, b::2], I16, True, True, ["HVa", "HVb", "hI"], ["#xA"], 80, 128)
         CP(T.HT[:, :], X[0:80, 0:256], ["#xA"], ["HT"], 256)
-        MM(X2[:, 0:256], CH[0:80, 1104:1232], T.HT[:, :], True, True, ["hPR", "HT"], ["#xB"], 128, 256)
-        TS(T.OFR[:, :], X2[:, 0:256], 2048.0, OP.add, ["#xB"], ["OFR"], 256)
+        MM(X2[:, 0:128], CH[0:80, 1104:1232], T.HT[:, 0::2], True, False, ["hPR", "HT"], ["#xB"], 128, 128)
+        MM(X2[:, 0:128], CH[0:80, 1360:1488], T.HT[:, 1::2], False, True, ["hPS", "HT"], ["#xB"], 128, 128)
+        for z in range(8):
+            MM(X2[:, 128:160], CH[64:80, 1488 + z * 128:1616 + z * 128], T.HT[64:80, z::8], z == 0, z == 7, ["hPS", "HT"], ["#xB"], 128, 32)
+        TS(T.OFR[:, 0:160], X2[:, 0:160], 2048.0, OP.add, ["#xB"], ["OFR"], 160)
         win = tab[:, 0:2064]
-        op("s", lambda: g.scalar.activation(T.XR[:, 2048:4096], win.indirect(T.OFR[:, 128:256]), FN.Copy), ["OFR", tk, tk + "z"], ["XR1"], 3072 * CY)
-        V(lambda e: e.tensor_copy(T.XR[:, 0:2048], win.indirect(T.OFR[:, 0:128])), ["OFR", tk, tk + "z"], ["XR0"], 3072)
+        for b in (1, 0):
+            for x0, ln in ((b * 1024, 1024), (2048 + b * 256, 256)):
+                xo, fo = T.XR[:, x0:x0 + ln], T.OFR[:, x0 // 16:(x0 + ln) // 16]
+                if b:
+                    op("s", lambda xo=xo, fo=fo: g.scalar.activation(xo, win.indirect(fo), FN.Copy), ["OFR", tk, tk + "z"], ["XR%d.%d" % (b, ln)], ln * 1.5 * CY + 0.07)
+                else:
+                    V(lambda e, xo=xo, fo=fo: e.tensor_copy(xo, win.indirect(fo)), ["OFR", tk, tk + "z"], ["XR%d.%d" % (b, ln)], ln * 1.5)
         for b in (0, 1):
             MM(X[0:80, b * 128:b * 128 + 128], T.TV[:, b::2], I16, True, True, ["TVa", "TVb", "hI"], ["#xA"], 80, 128)
-        CP(T.TVL[:, :], X[0:80, 0:256], ["#xA"], ["TVL"], 256)
+        S(T.TVL[:, :], X[0:80, 0:256], FN.Copy, ["#xA"], ["TVL"], 256)
         hot(0, 16, "a", hk)
         hot(128, 160, "b", hk)
         B, W = PS["kB"], PS["wA"]
         for b in (0, 1):
             for m in range(10):
-                MM(B[:, b * 128:b * 128 + 128], IB, T.XR[:, b * 2048 + m:(b + 1) * 2048:16], m == 0, m == 9, ["cI", "XR%d" % b], ["#kB"], 128, 128)
+                xs = T.XR[:, b * 1024 + m:(b + 1) * 1024:8] if m < 8 else T.XR[:, 2040 + b * 256 + m:2304 + b * 256:2]
+                MM(B[:, b * 128:b * 128 + 128], IB, xs, m == 0, m == 9, ["cI", "XR%d.%d" % (b, 1024 if m < 8 else 256)], ["#kB"], 128, 128)
         for b in (0, 1):
             TS(T.CMP[:, b * 128:b * 128 + 128], B[:, b * 128:b * 128 + 128], T.THF[:, 0:1], OP.is_ge, ["#kB", "THF"], ["CMP%d" % b], 128)
         MM(W[0:80, 0:256], CB[:, 1024:1104], T.CMP[:, :], True, True, ["CMP0", "CMP1", "cRC"], ["#wA"], 80, 256)
         TS(T.HVY[:, :], W[0:80, 0:256], 8.5, OP.is_ge, ["#wA"], ["HVY"], 256)
-        TTo(T.TM[:, :], T.TVL[:, :], T.HVY[:, :], OP.mult, ["TVL", "HVY"], ["TM"], 512)
+        TTo(T.TM[0:80, :], T.TVL[:, :], T.HVY[:, :], OP.mult, ["TVL", "HVY", "TMz"], ["TM"], 512)
         C = PS["wB"]
         z = 0
         for b in (0, 1):
@@ -543,16 +581,25 @@ def build(g, core, T, topo):
                 c1 = min(1280, c0 + 512)
                 bn = ("xA", "wA", "dA")[z % 3]
                 z += 1
-                MM(PS[bn][:, 0:c1 - c0], T.TM[:, b * 128:b * 128 + 128], T.RT[:, c0:c1], True, True, ["TM", "RT"], ["#" + bn], 128, c1 - c0)
-                TTo(T.TL[:, b * 1280 + c0:b * 1280 + c1], PS[bn][:, 0:c1 - c0], T.THR[:, 0:c1 - c0], OP.is_ge, ["#" + bn, "THR"], ["TL%d.%d" % (b, c0 // 512)], c1 - c0)
-        for gr in range(8):
-            for z, (m, b) in enumerate([(m, b) for b in (0, 1) for m in range(10)]):
-                col = m * 16 + gr * 2 + b
-                l0 = (m * 8 + gr) * 16
-                MM(C[:, gr * 16:gr * 16 + 16], T.OH[:, col * 128:col * 128 + 128], T.TL[:, b * 1280 + l0:b * 1280 + l0 + 16], z == 0, z == 19,
-                   ["OH%d" % col, "TL%d.%d" % (b, l0 // 512)], ["#wB"], 128, 16)
-        TTo(T.CS[:, 0:128], C[:, 0:128], T.MT0[:, :], OP.mult, ["#wB", "MT0"], ["CS"], 128)
-        TTo(T.DD[:, :], C[:, 0:128], T.CS[:, 1:129], OP.subtract, ["#wB", "CS", "CSz"], ["DD"], 128)
+                MM(PS[bn][:, 0:c1 - c0], T.TM[:, b * 128:b * 128 + 128], T.RT[:, c0:c1], True, True, ["TM", "TMz", "RT"], ["#" + bn], 128, c1 - c0)
+                S(T.TL[:, b * 1280 + c0:b * 1280 + c1], PS[bn][:, 0:c1 - c0], FN.Sigmoid, ["#" + bn, "CSz"], ["TL%d.%d" % (b, c0 // 512)], c1 - c0,
+                  bias=T.CS[:, 129:130], scale=200.0)
+        for b in (0, 1):
+            for th in (0, 1):
+                for gr in range(8):
+                    ms = [m for m in range(10) if (m in SHOT) == bool(th)]
+                    y = th * 256 + b * 128 + gr * 16
+                    for m in ms:
+                        col = m * 16 + gr * 2 + b
+                        l0 = (m * 8 + gr) * 16
+                        MM(C[:, y:y + 16], T.OH[:, col * 128:col * 128 + 128], T.TL[:, b * 1280 + l0:b * 1280 + l0 + 16], m == ms[0], m == ms[-1],
+                           ["OH%d" % col, "TL%d.%d" % (b, l0 // 512)], ["#wB"], 128, 16)
+        CP(T.C2[:, :], C[:, :], ["#wB"], ["C2"], 512)
+        C = PS["xB"]
+        for z in range(4):
+            MM(C[:, 0:128], CH[:, 1232:1360] if z > 1 else I16, T.C2[:, z * 128:z * 128 + 128], z == 0, z == 3, ["hDM", "hI", "C2"], ["#xB"], 128, 128)
+        TTo(T.CS[:, 0:128], C[:, 0:128], T.MT0[:, :], OP.mult, ["#xB", "MT0"], ["CS"], 128)
+        TTo(T.DD[:, :], C[:, 0:128], T.CS[:, 1:129], OP.subtract, ["#xB", "CS", "CSz"], ["DD"], 128)
         TS(T.MK[:, :], T.DD[:, :], 1.0, OP.min, ["DD"], ["MK"], 128, -512.0, OP.mult)
         MM(X[:, 0:128], T.MK[:, :], IB, True, True, ["MK", "cI"], ["#xA"], 128, 128)
         S(T.MKT[:, :], X[:, 0:128], FN.Copy, ["#xA"], ["MKT"], 128)
@@ -659,7 +706,7 @@ def schedule(ops):
                 if s < bt:
                     bt, bq = s, q
         lst = ready[bq]
-        pick, pp = None, -1.0
+        pick, pp = None, -1e9
         for i in lst:
             if max(free.get(bq, 0.0), tready[i]) <= bt + 0.1 and prio[i] > pp:
                 pick, pp = i, prio[i]

from concourse.mybir import dt, AluOpType, ActivationFunctionType
import comms_topo

OP = AluOpType
FN = ActivationFunctionType
BIG = float(2 ** 26)
REST = float(2041 * 8192)
F32, B16, H16, I32 = "float32", "bfloat16", "float16", "int32"
SCRATCH = {}
for _n, _p, _w, _t in (
        ("NB", 128, 1024, I32), ("XI", 128, 1024, I32), ("TO", 128, 2064, B16), ("TO1", 128, 2064, B16), ("TO2", 128, 2048, B16),
        ("TP0", 128, 2048, B16), ("TPn", 128, 2048, B16), ("TP1", 128, 2048, B16), ("EL0", 128, 2048, B16), ("ELn", 128, 2048, B16),
        ("EL1", 128, 2048, B16), ("TMP", 128, 2048, H16), ("ST", 128, 32, I32), ("SU", 128, 32, "uint16"), ("TH", 128, 1, I32),
        ("THF", 128, 1, F32), ("Q", 128, 256, B16), ("QR", 128, 4096, B16), ("ON", 128, 2048, B16), ("CB", 128, 2384, B16),
        ("CT", 128, 464, B16), ("CH", 128, 2512, H16), ("C2", 128, 512, H16), ("CF", 9, 1024, B16), ("CW", 9, 1408, H16),
        ("VS", 8, 2048, B16), ("VH", 8, 2048, H16), ("SELL", 128, 2048, B16), ("CBIG", 128, 256, B16), ("S8", 128, 8, B16),
        ("NEGI", 128, 128, B16), ("CR", 33, 512, B16), ("I128", 128, 128, B16), ("RT", 97, 1280, B16), ("MT0", 128, 128, B16),
        ("WT", 128, 384, B16), ("NT", 9, 3072, H16), ("X0B", 128, 256, H16), ("PT0", 128, 176, H16), ("PT1", 128, 176, H16),
        ("NPK0", 128, 128, F32), ("NPK1", 128, 128, F32), ("U", 128, 176, F32), ("PR", 128, 144, F32), ("V5", 128, 144, F32),
        ("TT", 128, 160, I32), ("HH", 128, 160, I32), ("EQ", 128, 384, B16), ("EW", 128, 384, B16), ("E1", 128, 192, B16),
        ("E2", 128, 96, B16), ("E3", 128, 64, B16), ("JS", 128, 128, F32), ("JR", 128, 16, I32), ("IL", 128, 32, H16),
        ("VV", 128, 176, F32), ("MI", 128, 160, F32), ("JP", 128, 240, H16), ("UJ", 128, 48, F32), ("WW", 128, 160, I32),
        ("TB", 128, 160, I32), ("TBP", 128, 160, F32), ("TV", 128, 160, H16), ("TVL", 80, 256, B16), ("HS", 128, 160, F32),
        ("HV", 128, 160, H16), ("WS", 128, 320, F32), ("HT", 80, 256, H16), ("OFR", 128, 256, "uint16"), ("XR", 128, 2560, B16),
        ("CMP", 128, 256, B16), ("HVY", 80, 256, B16), ("TM", 97, 256, B16), ("OH", 128, 20480, B16), ("TL", 128, 2560, B16),
        ("CS", 128, 132, F32), ("DD", 128, 128, F32), ("MK", 128, 128, B16), ("MKT", 128, 128, B16), ("MKP", 128, 128, B16),
        ("YN", 128, 256, H16), ("YM", 128, 256, H16), ("YP", 128, 256, H16), ("YK", 128, 1024, H16), ("YB", 128, 1536, H16),
        ("YR", 128, 512, F32)):
    SCRATCH[_n] = ("sbuf", [_p, _w], _t)
for _c in "01":
    for _n, _w, _t in (("NN", 256, H16), ("M", 256, F32), ("T", 256, I32), ("B", 256, I32), ("OF", 256, "uint16"), ("DV", 2560, B16),
                       ("AB", 4096, B16), ("XG", 2048, B16), ("BQ", 1280, B16), ("SB", 128, F32), ("L1", 128, F32), ("L2", 64, F32),
                       ("K", 32, I32), ("KD", 64, F32), ("SH", 32, I32), ("R", 32, I32), ("VL", 16, "uint16")):
        SCRATCH[_n + _c] = ("sbuf", [128, _w], _t)
BANKS = ("kA", "kB", "wA", "wB", "xA", "xB", "dA", "dB")
for _b in BANKS:
    SCRATCH[_b] = ("psum", [128, 512], F32)
NITEM = 7
NDMA = 14
SEMAPHORES = ["v", "s", "t", "gc", "aTP0", "aTPn", "aMK"] + ["d%d" % i for i in range(NDMA)]
SEMAPHORES += ["ri%d" % i for i in range(NITEM)] + ["lo%d" % i for i in range(NITEM)]

CY = 0.00104
TCY = 0.00075
LEAD = 6.0
SHOT = (1, 2, 3, 4)
HINT = {"vM1": -2.0, "vOF0": -5.0, "vBQ1": 1.0, "vNN0": -0.5, "t#kA": -0.5, "t#xB": 0.5, "sab0": -28.5, "vCSz": 13.0, "vYP": -8.0,
        "vOH": -7.0, "vhF": -20.0, "vWWe": -3.5, "vVL0": -2.5, "vMJ": -2.5, "vTVb": -2.0, "sXG0": -8.5, "vwP": -4.0, "sXG1": -0.5,
        "vMK": 7.0, "vcPa": 2.0, "vSH1": 16.0, "vWSb": -5.0, "vcE": 10.5, "vhPS": -6.0, "vD20": 1.0, "vPTu": -4.0, "vWWa": 1.5,
        "vNT": 1.5, "t#dA": 0.5, "vTHF": -0.5, "vJR": 1.0, "vJP": -2.0, "vTMz": 8.5, "vR1": 5.0, "vDD": 0.5}
ORDERS = {}


def items(x, T, topo):
    me = T.cores[x]
    n = len(T.cores)

    def via(dst, other):
        if not other and topo.may_write(me, dst):
            return None
        for c in topo.cores_of(me):
            if c != me and topo.may_write(c, dst) and (topo.die(c) != topo.die(me)) == bool(other):
                return c
        for c in topo.cores_of(me):
            if c != me and topo.may_write(c, dst):
                return c
        return None
    out = []
    d0, d1 = T.cores[(x - 1) % n], T.cores[(x - 2) % n]
    for h, c0 in ((0, 0), (1, 1024), (0, 512), (1, 1536)):
        out.append(("TO", c0, c0 + 512, "TP0", "aTP0", d0, via(d0, h)))
    for h in (0, 1):
        out.append(("TO", h * 1024, h * 1024 + 1024, "TPn", "aTPn", d1, via(d1, h)))
    out.append(("MKT", 0, 128, "MKP", "aMK", d1, via(d1, 0)))
    return out


def remote(g, T, topo, core, dst, out, src, rsem, lsem):
    rid, pid = topo.addr(dst, core)
    g.remote_dma(out, src, T.sem[rsem], T.sem[lsem], pid, rid, topo.mask(core, dst))


def hand_on(g, core, T, topo):
    todo = []
    for x in range(len(T.cores)):
        for k, it in enumerate(items(x, T, topo)):
            if it[6] == core:
                todo.append((k, it, len(topo.engines(T.cores[x], core))))
    for k, it, ne in todo:
        g.wait_ge(T.sem["ri%d" % k], ne)
        ap = T[it[3]][:, it[1]:it[2]]
        remote(g, T, topo, core, it[5], ap, ap, it[4], "lo%d" % k)
    for k, it, ne in todo:
        g.wait_ge(T.sem["lo%d" % k], len(topo.engines(core, it[5])))


def build(g, core, T, topo):
    ops = []
    lastw, reads, bank = {}, {}, {}
    bon = [0.0]

    def hint(q, W):
        if not W or q is None:
            return 0.0
        w = W[0].split(".")[0]
        for name in (w, w[:3], "".join(c for c in w if not c.isdigit())):
            if q + name in HINT:
                return HINT[q + name]
        return 0.0

    def op(q, fn, R, W, cost, kind="c", sem=None, val=1, lat=0.0):
        n = len(ops)
        deps, order = set(), set()
        for k in list(R) + list(W):
            if k[0] == "#":
                b = bank.setdefault(k, {})
                for e in b:
                    if e == q:
                        order.add(b[e][-1])
                    elif e != "last":
                        deps.update(b[e])
                b[q] = b[q] + [n] if b.get("last") == [q] else [n]
                b["last"] = [q]
        for k in R:
            if k[0] != "#":
                if k in lastw:
                    deps.add(lastw[k])
                reads.setdefault(k, []).append(n)
        for k in W:
            if k[0] != "#":
                if k in lastw:
                    deps.add(lastw[k])
                deps.update(reads.get(k, []))
                lastw[k] = n
                reads[k] = []
        deps.discard(n)
        order.discard(n)
        ops.append(dict(q=q, fn=fn, deps=deps, order=(order - deps if q == "t" else set()), cost=cost, lat=lat, kind=kind, sem=sem, val=val, bon=bon[0] + hint(q, W)))

    def V(fn, R, W, n):
        op("v", lambda: fn(g.vector), R, W, max(64, n) * CY + 0.03)

    def TS(out, a, s1, o0, R, W, n, s2=None, o1=None):
        if o1 is None:
            V(lambda e: e.tensor_scalar(out, a, s1, None, o0), R, W, n)
        else:
            V(lambda e: e.tensor_scalar(out, a, s1, s2, o0, o1), R, W, n)

    def TTo(out, a, b, o, R, W, n):
        V(lambda e: e.tensor_tensor(out, a, b, o), R, W, n)

    def CP(out, a, R, W, n):
        V(lambda e: e.tensor_copy(out, a), R, W, n)

    def fill(ap, c, R, W, n):
        V(lambda e: e.memset(ap, c), R, W, n)

    def S(out, a, f, R, W, n, **kw):
        op("s", lambda: g.scalar.activation(out, a, f, **kw), R, W, max(64, n) * CY + 0.05)

    def MM(out, l, r, st, sp, R, W, m, n):
        op("t", lambda: g.tensor.matmul(out, l, r, st, sp), R, W, max(min(64, m), n) * TCY + 0.01)

    def GC(fn, R, W, n):
        op("g", fn, R, W, 0.18 + 2 * n * CY)

    def iota(out, pat, base, R, W, n):
        GC(lambda: g.iota(out, pat, base, 0, allow_small_or_imprecise_dtypes=True), R, W, n)

    nd = [0]

    def DMA(q, out, a, R, W):
        s = "d%d" % nd[0]
        nd[0] += 1
        eng = g.sync if q == "y" else g.scalar
        op(q, lambda: eng.dma_start(out, a), R, W, 0.06, "d", s, 16, 2.5)

    PS = {b: T[b] for b in BANKS}

    DMA("y", T.ST[:, :], T.st[:, :], [], ["ST"])
    DMA("s", T.TO[:, 0:2048], T.ang[:, :], [], ["TO"])
    DMA("y", T.NB[:, :], T.nb[:, :], [], ["NB"])
    DMA("s", T.Q[:, :], T.q[:, :], [], ["Q"])
    DMA("y", T.TH[:, :], T.th[:, :], [], ["TH"])

    fill(T.ON[:, :], 1.0, [], ["ON"], 1024)
    fill(T.TO[:, 2048:2064], 0.0, [], ["TOz"], 64)
    fill(T.TO1[:, 2048:2064], 0.0, [], ["TO1z"], 64)

    def aff(out, src, pat, cmp, fv, base, cm, R, W):
        n = 1
        for p in pat:
            n *= p[1]
        GC(lambda: g.affine_select(out, src, pat, cmp, fv, base, cm), R, W, n)

    def eqs(b, c0, pat, base, key, rows=128, cm=1):
        n = 1
        for p in pat:
            n *= p[1]
        aff(b[0:rows, c0:c0 + n], T.ON[0:rows, 0:n], pat, OP.is_equal, 0.0, base, cm, ["ON"], [key])

    GC(lambda: g.iota(T.XI[:, 0:256], [[1, 256]], 0, 0), [], ["XI0"], 256)
    for z in range(1, 4):
        TS(T.XI[:, z * 256:z * 256 + 256], T.XI[:, 0:256], float(z * 256), OP.add, ["XI0"], ["XI%d" % z], 256)
    CB, CH, CF, CW, CT = T.CB, T.CH, T.CF, T.CW, T.CT
    hi = [[0, 8], [1, 2], [0, 8]]
    eqs(CB, 128, [[-1, 8], [-8, 2], [-16, 8]], 0, "cPM")
    eqs(CB, 0, [[-1, 128]], 0, "cI")
    iota(CT[:, 208:336], hi, 0, [], ["cHi"], 128)
    eqs(CB, 256, [[-1, 8], [-16, 8]], 0, "cA1")
    eqs(CB, 320, [[-1, 8], [-16, 8]], -8, "cB1")
    eqs(CF, 384, [[-1, 8], [0, 16]], 0, "cE0", 9)
    aff(CF[0:9, 0:128], CF[0:9, 384:512], [[0, 128]], OP.not_equal, 0.5, -8, 1, ["cE0"], ["cF0"])
    for z, kz in ((0, "cF"), (384, "cE")):
        TTo(CF[0:9, z + 256:z + 384], CF[0:9, z:z + 128], CT[0:9, 208:336], OP.mult, [kz + "0", "cHi"], [kz + "2"], 256)
        TTo(CF[0:9, z + 128:z + 256], CF[0:9, z:z + 128], CF[0:9, z + 256:z + 384], OP.subtract, [kz + "0", kz + "2"], [kz + "1"], 256)
    fill(T.CR[:, :], 0.0, [], ["CR"], 256)
    fill(T.CR[0:1, :], -16711680.0, ["CR"], ["CR"], 256)
    iota(T.CR[32:33, 0:256], [[0, 2], [1024, 8], [0, 16]], 0, ["CR"], ["CR"], 256)
    for z in (256, 384):
        iota(T.CR[32:33, z:z + 64], [[1024, 8], [0, 8]], 0, ["CR"], ["CR"], 64)
    aff(CT[:, 0:128], T.ON[:, 0:128], [[-16, 8], [0, 16]], OP.is_ge, 0.0, 0, 1, ["ON"], ["cT0"])
    aff(CB[:, 896:1024], CT[:, 0:128], [[16, 8], [0, 16]], OP.is_ge, 0.0, 15, -1, ["cT0"], ["cEB"])
    eqs(T.VS, 0, [[1, 16], [-16, 8], [-1, 16]], 0, "VS", 8, 16)
    iota(T.I128[:, :], [[1, 128]], -128, [], ["I128"], 128)
    eqs(T.RT, 0, [[-1, 80], [0, 16]], 0, "RT", 97)
    iota(T.RT[96:97, :], [[0, 80], [-1, 16]], -2, ["RT"], ["RT"], 1280)
    iota(T.MT0[:, :], [[0, 8], [1, 16]], 0, [], ["MT0"], 128)
    aff(CT[:, 128:208], T.ON[:, 0:80], [[0, 10], [-16, 8]], OP.is_ge, 0.0, 0, 1, ["ON"], ["cT1"])
    aff(CB[:, 1024:1104], CT[:, 128:208], [[0, 10], [16, 8]], OP.is_ge, 0.0, 15, -1, ["cT1"], ["cRC"])
    eqs(CB, 1104, [[-1, 8], [1000, 2], [-8, 8]], 0, "cPR", 80)
    eqs(CB, 1232, [[-1, 8], [1000, 2], [-8, 8]], -1000, "cPS", 80)
    for z in range(8):
        eqs(CB, 1360 + z * 128, [[-1, 8], [1000, 8], [-8, 2]], -64 - 1000 * z, "cPT%d" % z, 80)
    iota(CF[0:9, 768:896], [[0, 8], [-1, 16]], 0, [], ["cM0"], 128)
    aff(CF[0:9, 896:1024], CF[0:9, 768:896], [[0, 128]], OP.is_equal, 0.0, -8, 1, ["cM0"], ["cM1"])
    eqs(CT, 336, [[-1, 128]], -1, "cSF")
    eqs(T.SELL, 0, [[-1, 16], [-16, 8], [0, 16]], 0, "SELL")

    I16, IB = CH[:, 0:128], CB[:, 0:128]
    CP(T.SU[:, :], T.ST[:, :], ["ST"], ["SU"], 64)
    CP(CH[:, 128:256], CB[:, 128:256], ["cPM"], ["hPM"], 64)
    CP(CH[:, 0:128], IB, ["cI"], ["hI"], 64)
    fill(CB[:, 512:520], 0.0, [], ["cP1a"], 64)
    fill(CB[:, 760:768], 0.0, [], ["cP2a"], 64)
    TTo(CB[:, 768:896], IB, CT[:, 208:336], OP.mult, ["cI", "cHi"], ["cP3"], 256)
    TTo(CB[:, 384:512], IB, CB[:, 768:896], OP.subtract, ["cI", "cP3"], ["cP0"], 256)
    CP(CB[:, 520:640], CB[:, 384:504], ["cP0"], ["cP1"], 64)
    CP(CB[:, 640:760], CB[:, 776:896], ["cP3"], ["cP2"], 64)
    CP(CH[:, 384:896], CB[:, 384:896], ["cP0", "cP1", "cP1a", "cP2", "cP2a", "cP3"], ["hP4"], 256)
    CP(CH[:, 256:384], CB[:, 256:384], ["cA1", "cB1"], ["hF1"], 64)
    FK, EK = ["cF0", "cF1", "cF2"], ["cE0", "cE1", "cE2"]
    TS(CW[:, 0:384], CF[:, 0:384], 4.0, OP.mult, FK, ["wP"], 192)
    TS(CW[:, 384:768], CF[:, 0:384], 2.0, OP.mult, FK, ["wQ"], 192)
    TS(CW[:, 768:1152], CF[:, 384:768], 592.0, OP.mult, EK, ["wV"], 192)
    CP(CW[:, 1152:1280], CF[:, 384:512], EK, ["wE"], 64)
    for a in (0, 1, 2, 3, 6, 7, 8, 10, 11):
        CP(T.NT[:, a * 256:a * 256 + 256], T.ON[0:9, 0:256], ["ON"], ["NT%d" % a], 128)
    TS(T.CBIG[:, :], CB[:, 128:384], BIG, OP.mult, ["cPM", "cA1", "cB1"], ["CBIG"], 128)
    TS(T.S8[:, :], CB[:, 896:1024:16], 8192.0, OP.mult, ["cEB"], ["S8"], 64)
    TS(T.NEGI[:, :], IB, -1.0, OP.mult, ["cI"], ["NEGI"], 64)
    QE, QO = ["QR%d" % k for k in range(0, 16, 2)], ["QR%d" % k for k in range(1, 16, 2)]
    for k in list(range(0, 16, 2)) + list(range(1, 16, 2)):
        if k % 4 < 2:
            CP(T.QR[:, k::16], T.Q[:, :], ["Q"], ["QR%d" % k], 128)
        else:
            S(T.QR[:, k::16], T.Q[:, :], FN.Copy, ["Q"], ["QR%d" % k], 256)
    QA = QE + QO
    CP(T.VH[:, :], T.VS[:, :], ["VS"], ["VH"], 1024)

    def late_constants():
        CP(CH[0:80, 1104:1232], CB[0:80, 1104:1232], ["cPR"], ["hPR"], 64)
        CP(CH[0:80, 1360:2512], CB[0:80, 1232:2384], ["cPS"] + ["cPT%d" % z for z in range(8)], ["hPS"], 576)
        TTo(CW[:, 1280:1408], CF[:, 384:512], CF[:, 896:1024], OP.add, EK + ["cM1"], ["wM"], 256)
        TS(T.MT0[:, :], T.MT0[:, :], 1.0, OP.min, ["MT0"], ["MT0"], 64)
        CP(T.THF[:, :], T.TH[:, :], ["TH"], ["THF"], 64)
        fill(T.VV[:, 0:16], 0.0, [], ["VV0"], 64)
        fill(T.VV[:, 160:176], 0.0, [], ["VV10"], 64)
        TTo(CH[:, 1232:1360], IB, CT[:, 336:464], OP.subtract, ["cI", "cSF"], ["hDM"], 256)
        fill(T.TM[:, :], 0.0, [], ["TMz"], 64)
        fill(T.TM[96:97, :], 1.0, ["TMz"], ["TMz"], 64)
        fill(T.CS[:, 128:132], 0.0, [], ["CSz"], 64)
        fill(T.CS[:, 129:130], 100.0, ["CSz"], ["CSz"], 64)
        x = 0
        for L in range(3, 11):
            for i in range(max(1, L - 5), min(5, L - 1) + 1):
                fill(T.WT[:, x:x + 16], float(25 - (i - 1) * 5 - (L - i - 1)), [], ["WT%d" % x], 64)
                x += 16

    n = len(T.cores)
    r = T.rank_of(core)
    its = items(r, T, topo)

    def send(k):
        buf, c0, c1, land, asem, dst, rel = its[k]

        def fn():
            if rel is None:
                remote(g, T, topo, core, dst, T[land][:, c0:c1], T[buf][:, c0:c1], asem, "lo%d" % k)
            else:
                remote(g, T, topo, core, rel, T[land][:, c0:c1], T[buf][:, c0:c1], "ri%d" % k, "lo%d" % k)
        op("g", fn, [buf], [], 0.5, "r", "lo%d" % k, len(topo.engines(core, dst if rel is None else rel)))

    def arrive(land, asem, giver, lat, after):
        tot = 0
        for it in items(giver, T, topo):
            if it[4] == asem:
                tot += len(topo.engines(T.cores[giver] if it[6] is None else it[6], core))
        op(None, None, after, [land], 0.0, "x", asem, tot, lat)
    for k in range(6):
        send(k)
    arrive("TP0", "aTP0", (r + 1) % n, 14.0, ["TO"])
    arrive("TPn", "aTPn", (r + 2) % n, 25.0, ["TO"])

    NB = T.NB[:, 0:1024]

    def nt(c, a):
        return 0 if a == 0 else (a if c == 0 else 5 + a)

    def NTs(s, rows=9):
        return T.NT[0:rows, s * 256:s * 256 + 256]

    def start(t):
        P = "PT%d" % t
        vl = T.SU[:, t * 16:t * 16 + 16]
        V(lambda e: e.tensor_copy(T.X0B[:, :], T.XI[:, 0:1024].indirect(vl)), ["XI0", "XI1", "XI2", "XI3", "SU"], ["X0B"], 384)
        X = PS["xA"]
        MM(X[0:8, 0:256], CH[:, 128:136], T.X0B[:, :], True, True, ["hPM", "X0B"], ["#xA"], 8, 256)
        for b in (0, 1):
            MM(X[:, 256 + b * 8:264 + b * 8], T.X0B[:, b * 128:b * 128 + 128], CH[:, 128:136], True, True, ["hPM", "X0B"], ["#xA"], 128, 8)
        CP(T.NT[0:8, 0:256], X[0:8, 0:256], ["#xA"], ["NT0"], 256)
        for b in (0, 1):
            CP(T[P][:, 80 + b:96:2], X[:, 256 + b * 8:264 + b * 8], ["#xA"], [P + "s5"], 64)
        V(lambda e: e.tensor_copy(T.NN0[:, :], NB.indirect(vl)), ["NB", "SU"], ["NN0"], 384)

    def step(t, c, a, tab, tkey):
        C = str(c)
        P = "PT%d" % t
        bon[0] = LEAD * (1 - c)
        kb, wb, xb, db = ("kA", "wA", "xA", "dA") if c == 0 else ("kB", "wB", "xB", "dB")
        K, W, X, D = PS[kb], PS[wb], PS[xb], PS[db]
        KB, WB, XB, DB = "#" + kb, "#" + wb, "#" + xb, "#" + db
        nn, nnk = (T.NN0, "NN0") if a == 0 else (T["NN" + C], "NN" + C)

        def sl(i):
            return 5 + i if c == 0 else 5 - i
        if a == 0:
            w = 128
            p0 = 384 + 256 * c
            MM(X[:, 0:128], CH[:, p0:p0 + 128], nn[:, 0::2], True, False, ["hP4", nnk], [XB], 128, 128)
            MM(X[:, 0:128], CH[:, p0 + 128:p0 + 256], nn[:, 1::2], False, True, ["hP4", nnk], [XB], 128, 128)
            E, O = T.NT[:, 0:256:2], T.NT[:, 1:256:2]
            MM(W[:, 0:128], CW[:, 128:256], E, True, False, ["wP", "NT0"], [WB], 128, 128)
            MM(W[:, 0:128], CW[:, 256:384], O, False, True, ["wP", "NT0"], [WB], 128, 128)
            for z, (q0, src) in enumerate(((512, E), (640, O), (896, E), (1024, O))):
                MM(W[:, 256:384], CW[:, q0:q0 + 128], src, z == 0, z == 3, ["wQ", "wV", "NT0"], [WB], 128, 128)
            S(T["NPK" + C][:, :], X[:, 0:128], FN.Copy, [XB], ["NPK" + C], 128)
            src, sk = T["NPK" + C][:, :], "NPK" + C
            parts = ((1024, 512, "s"), (1536, 512, "s"), (0, 512, "v"), (512, 512, "v"))
        else:
            w = 256
            V(lambda e: e.tensor_copy(nn[:, :], NB.indirect(T["VL" + C][:, 0:16])), ["NB", "VL" + C], [nnk], 384)
            s0, s1 = nt(c, a - 1), nt(c, a)
            MM(W[:, 0:256], CW[:, 0:128], NTs(s0), True, True, ["wP", "NT%d" % s0], [WB], 128, 256)
            MM(W[:, 256:512], CW[:, 384:512], NTs(s0), True, False, ["wQ", "NT%d" % s0], [WB], 128, 256)
            MM(W[:, 256:512], CW[0:8, 768:896], NTs(s1, 8), False, True, ["wV", "NT%d" % s1], [WB], 128, 256)
            src, sk = nn[:, :], nnk
            parts = tuple((z, 512, "s") for z in (2560, 3072, 3584)) + tuple((z, 512, "v") for z in range(0, 2560, 512))
        TTo(T["M" + C][:, 0:w], src, W[:, 0:w], OP.mult, [sk, WB], ["M" + C], w)
        TTo(T["T" + C][:, 0:w], T["M" + C][:, 0:w], W[:, 256:256 + w], OP.add, ["M" + C, WB], ["T" + C], w)
        TS(T["B" + C][:, 0:w], T["T" + C][:, 0:w], 4, OP.arith_shift_right, ["T" + C], ["B" + C], w, 2047, OP.bitwise_and)
        CP(T["OF" + C][:, 0:w], T["B" + C][:, 0:w], ["B" + C], ["OF" + C], w)
        win = tab[:, 0:2048]
        dv, ab, xg = T["DV" + C], T["AB" + C], T["XG" + C]

        def keys(nm, p, ln):
            return ["%s%s.%d" % (nm, C, z) for z in range(p // 512, (p + ln) // 512)]

        def qv(p, ln):
            return T.QR[:, 2 * p:2 * p + 2 * ln:2] if a == 0 else T.QR[:, p:p + ln]
        QK = QE if a == 0 else QA
        for p, ln, e in parts:
            off = T["OF" + C][:, p // 16:(p + ln) // 16]
            if e == "v":
                V(lambda en, p=p, ln=ln, off=off: en.tensor_tensor(dv[:, p:p + ln], win.indirect(off), qv(p, ln), OP.subtract),
                  ["OF" + C, tkey] + QK, keys("dv", p, ln), ln * 1.5)
            else:
                op("s", lambda p=p, ln=ln, off=off: g.scalar.activation(xg[:, p % 2048:p % 2048 + ln], win.indirect(off), FN.Copy),
                   ["OF" + C, tkey], keys("XG", p % 2048, ln), ln * 1.5 * CY + 0.07)
        MM(K[:, 0:256], T.ON[0:33, 0:128], T.CR[:, 256 * (a == 0):256 * (a == 0) + 256], True, False, ["ON", "CR"], [KB], 128, 256)
        pc, pw, bc = (256 + 64 * c, 64, 128 + 64 * c) if a == 0 else (128, 128, 0)
        for b in (0, 1):
            MM(K[:, b * 128:b * 128 + pw], nn[:, b * 128:b * 128 + 128], CH[:, pc:pc + pw], False, False, [nnk, "hPM", "hF1"], [KB], 128, pw)
        for p, ln, e in parts:
            if e == "v":
                S(ab[:, p:p + ln], dv[:, p:p + ln], FN.Abs, keys("dv", p, ln), keys("ab", p, ln), ln)
            else:
                MM(D[:, :], IB, xg[:, p % 2048:p % 2048 + 512], True, False, ["cI"] + keys("XG", p % 2048, 512), [DB], 128, 512)
                MM(D[:, :], T.NEGI[:, :], qv(p, 512), False, True, ["NEGI"] + QK, [DB], 128, 512)
                S(ab[:, p:p + 512], D[:, :], FN.Abs, [DB], keys("ab", p, 512), 512)

        def score(b, last):
            stp = 8 if a == 0 else 16
            base = b * 128 * stp
            for k in range(stp):
                col = b * 128 + (k * 8 if a == 0 else (k % 8) * 16 + (k // 8) * 8)
                MM(K[:, col:col + 8], ab[:, base + k:base + 128 * stp:stp], T.S8[:, :], False, last and k == stp - 1,
                   keys("ab", base, 128 * stp) + ["S8"], [KB], 128, 8)
        score(0, False)
        BQ = T["BQ" + C]
        for j in range(a + 1):
            s = nt(c, j)
            x0, j0 = (j % 2) * 256, j * 256
            MM(X[:, x0:x0 + 256], CW[0:8, 1152:1280], NTs(s, 8), True, True, ["wE", "NT%d" % s], [XB], 128, 256)
            bk = "BQ%s%d" % (C, j)
            TTo(BQ[:, j0:j0 + 256], nn[:, :], X[:, x0:x0 + 256], OP.is_equal, [nnk, XB], [bk], 256)
            for b in (0, 1):
                MM(K[:, b * 128:b * 128 + pw], BQ[:, j0 + b * 128:j0 + b * 128 + 128], T.CBIG[:, bc:bc + pw], False, False, [bk, "CBIG"], [KB], 128, pw)
        score(1, True)
        KD = T["KD" + C]
        TS(KD[:, 0:16], T[P][:, sl(a) * 16:sl(a) * 16 + 16], REST, OP.add, [P + "s%d" % sl(a)], ["KR" + C], 64)
        h = 32 if a == 0 else 64
        SBt, L1, L2, Kt, Rt, SHt = T["SB" + C], T["L1" + C], T["L2" + C], T["K" + C], T["R" + C], T["SH" + C]
        for b in (0, 1):
            S(SBt[:, b * 64:b * 64 + h], K[:, b * 128 + h:b * 128 + 2 * h], FN.Copy, [KB], ["SB%s%d" % (C, b)], h)
        for b in (0, 1):
            TTo(L1[:, b:2 * h:2], K[:, b * 128:b * 128 + h], SBt[:, b * 64:b * 64 + h], OP.min, [KB, "SB%s%d" % (C, b)], ["L1%s%d" % (C, b)], h)
        TTo(L2[:, 0:h], L1[:, 0:h], L1[:, h:2 * h], OP.min, ["L1%s0" % C, "L1%s1" % C], ["L2" + C], 2 * h)
        TTo(Kt[:, 0:h // 2], L2[:, 0:h // 2], L2[:, h // 2:h], OP.min, ["L2" + C], ["K" + C], h)
        TTo(Kt[:, 0:16], Kt[:, 0:16], KD[:, 0:16], OP.min, ["K" + C, "KR" + C], ["K" + C], 64)
        ns = sl(a + 1)
        out, ok = T[P][:, ns * 16:ns * 16 + 16], P + "s%d" % ns
        if a == 0:
            TS(Rt[:, 0:16], Kt[:, 0:16], 1023, OP.bitwise_and, ["K" + C], ["R" + C], 64)
            CP(out, Rt[:, 0:16], ["R" + C], [ok], 64)
        else:
            TS(SHt[:, :], Kt[:, :], 13, OP.arith_shift_right, ["K" + C], ["SH" + C], 64)
            TS(Rt[:, :], Kt[:, :], 1023, OP.bitwise_and, ["K" + C], ["R" + C], 64)
            TTo(KD[:, 16:32], SHt[:, 0:16], SHt[:, 16:32], OP.is_gt, ["SH" + C], ["SL" + C], 64)
            TTo(KD[:, 32:48], Rt[:, 16:32], Rt[:, 0:16], OP.subtract, ["R" + C], ["DF" + C], 64)
            TTo(KD[:, 48:64], KD[:, 32:48], KD[:, 16:32], OP.mult, ["DF" + C, "SL" + C], ["D2" + C], 64)
            TTo(out, Rt[:, 0:16], KD[:, 48:64], OP.add, ["R" + C, "D2" + C], [ok], 64)
        if a < 4:
            s = nt(c, a + 1)
            for b in (0, 1):
                MM(X[0:8, b * 128:b * 128 + 128], T[P][:, ns * 16 + b:ns * 16 + 16:2], I16, True, True, [ok, "hI"], [XB], 8, 128)
            CP(NTs(s, 8), X[0:8, 0:256], [XB], ["NT%d" % s], 256)
            for i in range(16):
                MM(X[:, 256:272], T.VH[:, i * 128:i * 128 + 128], T.NT[0:8, s * 256 + i:s * 256 + 256:16], i == 0, i == 15, ["VH", "NT%d" % s], [XB], 128, 16)
            CP(T["VL" + C][:, :], X[:, 256:272], [XB], ["VL" + C], 64)
        bon[0] = 0.0

    def lesser(el, tab, tk):
        TS(T.TMP[:, :], tab[:, 0:2048], 0.75, OP.mult, [tk], ["TMP"], 1024, 1024.375, OP.add)
        TS(T[el][:, :], T.TMP[:, :], -1024.0, OP.add, ["TMP"], [el], 1024)

    def lessen(tab, tk, mk, el, out, okey, banks):
        for qd in range(4):
            b = banks[qd % len(banks)]
            B = PS[b]
            MM(B[:, :], IB, tab[:, qd * 512:qd * 512 + 512], True, False, ["cI", tk], ["#" + b], 128, 512)
            for z in range(4):
                tt = (qd * 4 + z) * 128
                MM(B[:, z * 128:z * 128 + 128], T.SELL[:, tt:tt + 128], T[mk][:, :], False, z == 3, ["SELL", mk], ["#" + b], 128, 128)
            TTo(out[:, qd * 512:qd * 512 + 512], B[:, :], T[el][:, qd * 512:qd * 512 + 512], OP.max, ["#" + b, el], ["%s%d" % (okey, qd)], 512)

    def hot(c0, c1, kz, hk):
        TS(T.WW[:, c0:c1], T.HH[:, c0:c1], 127, OP.bitwise_and, hk, ["WW" + kz], c1 - c0)
        TS(T.WS[:, c0:c1], T.WW[:, c0:c1], -128.0, OP.add, ["WW" + kz], ["WS" + kz], c1 - c0)
        if kz == "e":
            S(T.WS[:, 160 + c0:160 + c1], T.WS[:, c0:c1], FN.Copy, ["WSe"], ["WB"], c1 - c0, bias=100.0, scale=200.0)
        for col in sorted(range(c0, c1), key=lambda z: (z % 2, z % 16, z)):
            o = T.OH[:, col * 128:col * 128 + 128]
            if col // 16 in SHOT:
                S(o, T.I128[:, :], FN.Sigmoid, ["I128", "WB"], ["OH%d" % col], 128, bias=T.WS[:, 160 + col:161 + col], scale=-200.0)
            else:
                TS(o, T.I128[:, :], T.WS[:, col:col + 1], OP.is_equal, ["I128", "WS" + kz], ["OH%d" % col], 64)

    def rings(t, tab, tk):
        P = "PT%d" % t
        pt, JS = T[P], T.JS
        pk = [P + "s%d" % i for i in range(11)]
        uk, hw = [P + "u%d" % i for i in range(3)], ["HHe", "HHx", "HHy"]
        for z, (c0, c1, kk) in enumerate(((16, 160, pk[1:10]), (0, 16, pk[0:1]), (160, 176, pk[10:11]))):
            TS(T.U[:, c0:c1], pt[:, c0:c1], 2.0, OP.mult, kk, [uk[z]], c1 - c0, 1.0, OP.add)
        for z, (c0, c1, kk, ku) in enumerate(((16, 128, pk[1:10], uk[0:1]), (0, 16, pk[0:3], uk[0:2]), (128, 144, pk[8:11], [uk[0], uk[2]]))):
            TTo(T.PR[:, c0:c1], T.U[:, c0:c1], T.U[:, c0 + 32:c1 + 32], OP.mult, ku, ["PR%d" % z], 2 * (c1 - c0))
            TS(T.V5[:, c0:c1], pt[:, c0 + 16:c1 + 16], 592.0, OP.mult, kk, ["V5%d" % z], c1 - c0)
            TTo(T.TT[:, c0:c1], T.PR[:, c0:c1], T.V5[:, c0:c1], OP.add, ["PR%d" % z, "V5%d" % z], ["TT%d" % z], 2 * (c1 - c0))
            TS(T.HH[:, c0:c1], T.TT[:, c0:c1], 4, OP.arith_shift_right, ["TT%d" % z], [hw[z]], c1 - c0, 2047, OP.bitwise_and)
        hot(16, 128, "e", ["HHe"])
        x = 0
        ek = []
        for L in range(3, 11):
            i0 = max(1, L - 5)
            m = (min(5, L - 1) - i0 + 1) * 16
            a0, b0 = (5 + i0) * 16, (5 + i0 - L) * 16
            TTo(T.EQ[:, x:x + m], pt[:, a0:a0 + m], pt[:, b0:b0 + m], OP.is_equal, pk, ["EQ%d" % L], 2 * m)
            ek.append("EQ%d" % L)
            x += m
        TTo(T.EW[:, :], T.EQ[:, :], T.WT[:, :], OP.mult, ek + ["WT%d" % z for z in range(0, 384, 16)], ["EW"], 768)
        TTo(T.E1[:, :], T.EW[:, 0:192], T.EW[:, 192:384], OP.max, ["EW"], ["E1"], 384)
        TTo(T.E2[:, :], T.E1[:, 0:96], T.E1[:, 96:192], OP.max, ["E1"], ["E2"], 192)
        TTo(T.E3[:, 0:48], T.E2[:, 0:48], T.E2[:, 48:96], OP.max, ["E2"], ["E3"], 96)
        TTo(T.E3[:, 48:64], T.E3[:, 0:16], T.E3[:, 16:32], OP.max, ["E3"], ["E4"], 64)
        JW, JF, JI, JU, JL, JJ, VJ, PJ = [JS[:, z * 16:z * 16 + 16] for z in range(8)]
        TTo(JW, T.E3[:, 48:64], T.E3[:, 32:48], OP.max, ["E3", "E4"], ["JW"], 64)
        TS(JF, JW, 0.5, OP.is_ge, ["JW"], ["JF"], 64)
        TS(T.JR[:, :], JW, -0.2, OP.mult, ["JW"], ["JR"], 64, 5.6, OP.add)
        TTo(JI, T.JR[:, :], JF, OP.mult, ["JR", "JF"], ["JI"], 64)
        TS(JU, T.JR[:, :], -4.0, OP.mult, ["JR"], ["JU"], 64, 31.0, OP.add)
        TTo(JL, JU, JW, OP.subtract, ["JU", "JW"], ["JL"], 64)
        TTo(T.IL[:, 16:32], JL, JF, OP.mult, ["JL", "JF"], ["ILl"], 64)
        TTo(JJ, T.IL[:, 16:32], JI, OP.subtract, ["ILl", "JI"], ["JJ"], 64)
        for m in range(0, 5):
            z = (5 + m) * 16
            TS(T.VV[:, z:z + 16], JI, m + 0.5, OP.is_ge, ["JI"], ["VV%d" % (5 + m)], 64)
            if m:
                z = (5 - m) * 16
                TS(T.VV[:, z:z + 16], JJ, m + 0.5, OP.is_ge, ["JJ"], ["VV%d" % (5 - m)], 64)
        vk = ["VV%d" % i for i in range(11)]
        MI, MJ = T.MI[:, 0:80], T.MI[:, 80:160]
        TTo(MI, T.VV[:, 80:160], T.VV[:, 96:176], OP.subtract, vk, ["MI"], 160)
        TTo(MJ, T.VV[:, 16:96], T.VV[:, 0:80], OP.subtract, vk, ["MJ"], 160)
        TTo(T.JP[:, 0:80], MI, pt[:, 80:160], OP.mult, ["MI"] + pk, ["JP0"], 160)
        TTo(T.JP[:, 80:160], MI, pt[:, 96:176], OP.mult, ["MI"] + pk, ["JP1"], 160)
        TTo(T.JP[:, 160:240], MJ, pt[:, 16:96], OP.mult, ["MJ"] + pk, ["JP2"], 160)
        J = PS["kA"]
        for z in range(3):
            for k in range(5):
                MM(J[:, z * 16:z * 16 + 16], I16, T.JP[:, z * 80 + k * 16:z * 80 + k * 16 + 16], k == 0, k == 4, ["hI", "JP%d" % z], ["#kA"], 128, 16)
        TS(T.UJ[:, :], J[:, 0:48], 2.0, OP.mult, ["#kA"], ["UJ"], 64, 1.0, OP.add)
        TS(VJ, J[:, 16:32], 592.0, OP.mult, ["#kA"], ["VJ"], 64)
        TTo(PJ, T.UJ[:, 0:16], T.UJ[:, 32:48], OP.mult, ["UJ"], ["PJ"], 64)
        TTo(T.TT[:, 144:160], PJ, VJ, OP.add, ["PJ", "VJ"], ["TTb"], 64)
        TS(T.HH[:, 144:160], T.TT[:, 144:160], 4, OP.arith_shift_right, ["TTb"], ["HHb"], 64, 2047, OP.bitwise_and)
        hk = hw + ["HHb"]
        TS(T.HS[:, :], T.HH[:, :], -2048.0, OP.add, hk, ["HS"], 160)
        TTo(T.HV[:, 0:144], T.HS[:, 0:144], T.VV[:, 16:160], OP.mult, ["HS"] + vk, ["HVa"], 288)
        TTo(T.HV[:, 144:160], T.HS[:, 144:160], T.VV[:, 80:96], OP.mult, ["HS"] + vk, ["HVb"], 64)
        TS(T.TB[:, :], T.HH[:, :], 7, OP.arith_shift_right, hk, ["TB"], 160)
        TS(T.TBP[:, :], T.TB[:, :], 2.0, OP.add, ["TB"], ["TBP"], 160)
        TTo(T.TV[:, 0:144], T.TBP[:, 0:144], T.VV[:, 16:160], OP.mult, ["TBP"] + vk, ["TVa"], 288)
        TTo(T.TV[:, 144:160], T.TBP[:, 144:160], T.VV[:, 80:96], OP.mult, ["TBP"] + vk, ["TVb"], 64)
        X, X2 = PS["xA"], PS["xB"]
        for b in (0, 1):
            MM(X[0:80, b * 128:b * 128 + 128], T.HV[:, b::2], I16, True, True, ["HVa", "HVb", "hI"], ["#xA"], 80, 128)
        CP(T.HT[:, :], X[0:80, 0:256], ["#xA"], ["HT"], 256)
        MM(X2[:, 0:128], CH[0:80, 1104:1232], T.HT[:, 0::2], True, False, ["hPR", "HT"], ["#xB"], 128, 128)
        MM(X2[:, 0:128], CH[0:80, 1360:1488], T.HT[:, 1::2], False, True, ["hPS", "HT"], ["#xB"], 128, 128)
        for z in range(8):
            MM(X2[:, 128:160], CH[64:80, 1488 + z * 128:1616 + z * 128], T.HT[64:80, z::8], z == 0, z == 7, ["hPS", "HT"], ["#xB"], 128, 32)
        TS(T.OFR[:, 0:160], X2[:, 0:160], 2048.0, OP.add, ["#xB"], ["OFR"], 160)
        win = tab[:, 0:2064]
        for b in (1, 0):
            for x0, ln in ((b * 1024, 1024), (2048 + b * 256, 256)):
                xo, fo = T.XR[:, x0:x0 + ln], T.OFR[:, x0 // 16:(x0 + ln) // 16]
                if b:
                    op("s", lambda xo=xo, fo=fo: g.scalar.activation(xo, win.indirect(fo), FN.Copy), ["OFR", tk, tk + "z"], ["XR%d.%d" % (b, ln)], ln * 1.5 * CY + 0.07)
                else:
                    V(lambda e, xo=xo, fo=fo: e.tensor_copy(xo, win.indirect(fo)), ["OFR", tk, tk + "z"], ["XR%d.%d" % (b, ln)], ln * 1.5)
        for b in (0, 1):
            MM(X[0:80, b * 128:b * 128 + 128], T.TV[:, b::2], I16, True, True, ["TVa", "TVb", "hI"], ["#xA"], 80, 128)
        S(T.TVL[:, :], X[0:80, 0:256], FN.Copy, ["#xA"], ["TVL"], 256)
        hot(0, 16, "a", hk)
        hot(128, 160, "b", hk)
        B, W = PS["kB"], PS["wA"]
        for b in (0, 1):
            for m in range(10):
                xs = T.XR[:, b * 1024 + m:(b + 1) * 1024:8] if m < 8 else T.XR[:, 2040 + b * 256 + m:2304 + b * 256:2]
                MM(B[:, b * 128:b * 128 + 128], IB, xs, m == 0, m == 9, ["cI", "XR%d.%d" % (b, 1024 if m < 8 else 256)], ["#kB"], 128, 128)
        for b in (0, 1):
            TS(T.CMP[:, b * 128:b * 128 + 128], B[:, b * 128:b * 128 + 128], T.THF[:, 0:1], OP.is_ge, ["#kB", "THF"], ["CMP%d" % b], 128)
        MM(W[0:80, 0:256], CB[:, 1024:1104], T.CMP[:, :], True, True, ["CMP0", "CMP1", "cRC"], ["#wA"], 80, 256)
        TS(T.HVY[:, :], W[0:80, 0:256], 8.5, OP.is_ge, ["#wA"], ["HVY"], 256)
        TTo(T.TM[0:80, :], T.TVL[:, :], T.HVY[:, :], OP.mult, ["TVL", "HVY", "TMz"], ["TM"], 512)
        C = PS["wB"]
        z = 0
        for b in (0, 1):
            for c0 in range(0, 1280, 512):
                c1 = min(1280, c0 + 512)
                bn = ("xA", "wA", "dA")[z % 3]
                z += 1
                MM(PS[bn][:, 0:c1 - c0], T.TM[:, b * 128:b * 128 + 128], T.RT[:, c0:c1], True, True, ["TM", "TMz", "RT"], ["#" + bn], 128, c1 - c0)
                S(T.TL[:, b * 1280 + c0:b * 1280 + c1], PS[bn][:, 0:c1 - c0], FN.Sigmoid, ["#" + bn, "CSz"], ["TL%d.%d" % (b, c0 // 512)], c1 - c0,
                  bias=T.CS[:, 129:130], scale=200.0)
        for b in (0, 1):
            for th in (0, 1):
                for gr in range(8):
                    ms = [m for m in range(10) if (m in SHOT) == bool(th)]
                    y = th * 256 + b * 128 + gr * 16
                    for m in ms:
                        col = m * 16 + gr * 2 + b
                        l0 = (m * 8 + gr) * 16
                        MM(C[:, y:y + 16], T.OH[:, col * 128:col * 128 + 128], T.TL[:, b * 1280 + l0:b * 1280 + l0 + 16], m == ms[0], m == ms[-1],
                           ["OH%d" % col, "TL%d.%d" % (b, l0 // 512)], ["#wB"], 128, 16)
        CP(T.C2[:, :], C[:, :], ["#wB"], ["C2"], 512)
        C = PS["xB"]
        for z in range(4):
            MM(C[:, 0:128], CH[:, 1232:1360] if z > 1 else I16, T.C2[:, z * 128:z * 128 + 128], z == 0, z == 3, ["hDM", "hI", "C2"], ["#xB"], 128, 128)
        TTo(T.CS[:, 0:128], C[:, 0:128], T.MT0[:, :], OP.mult, ["#xB", "MT0"], ["CS"], 128)
        TTo(T.DD[:, :], C[:, 0:128], T.CS[:, 1:129], OP.subtract, ["#xB", "CS", "CSz"], ["DD"], 128)
        TS(T.MK[:, :], T.DD[:, :], 1.0, OP.min, ["DD"], ["MK"], 128, -512.0, OP.mult)
        MM(X[:, 0:128], T.MK[:, :], IB, True, True, ["MK", "cI"], ["#xA"], 128, 128)
        S(T.MKT[:, :], X[:, 0:128], FN.Copy, ["#xA"], ["MKT"], 128)

    def show(t):
        P = "PT%d" % t
        pt = T[P]
        D, E = PS["dA"], PS["dB"]
        TTo(T.IL[:, 0:16], T.JS[:, 32:48], T.JS[:, 16:32], OP.add, ["JI", "JF"], ["ILi"], 64)
        for b in (0, 1):
            MM(D[0:8, b * 128:b * 128 + 128], pt[:, 160 + b:176:2], I16, True, True, [P + "s10", "hI"], ["#dA"], 8, 128)
        for b in (0, 1):
            MM(D[0:8, 256 + b * 128:384 + b * 128], T.IL[:, b:16:2], I16, True, True, ["ILi", "hI"], ["#dA"], 8, 128)
        for b in (0, 1):
            MM(E[0:8, b * 128:b * 128 + 128], T.IL[:, 16 + b:32:2], I16, True, True, ["ILl", "hI"], ["#dB"], 8, 128)
        CP(NTs(5, 8), D[0:8, 0:256], ["#dA"], ["NT5"], 256)
        CP(NTs(10, 8), D[0:8, 256:512], ["#dA"], ["NT10"], 256)
        CP(NTs(11, 8), E[0:8, 0:256], ["#dB"], ["NT11"], 256)
        for z in (0, 1):
            MM(D[:, z * 256:z * 256 + 256], CW[:, 1280:1408], NTs(10 + z), True, True, ["wM", "NT%d" % (10 + z)], ["#dA"], 128, 256)
        for i in range(6):
            MM(E[:, 0:256], T.VH[:, i * 128:i * 128 + 128], NTs(i, 8), i == 0, i == 5, ["VH", "NT%d" % i], ["#dB"], 128, 256)
        R1, R2 = D[:, 0:256], D[:, 256:512]
        TS(T.YN[:, :], R1, 0.5, OP.is_le, ["#dA"], ["YN"], 256)
        TS(T.YM[:, :], R1, 0.5, OP.is_ge, ["#dA"], ["YM"], 256)
        TTo(T.YP[:, :], T.YN[:, :], R2, OP.mult, ["#dA", "YN"], ["YP"], 256)
        TS(T.YB[:, 256:512], R2, 0.5, OP.is_le, ["#dA"], ["YB1"], 256, -1.0, OP.mult)
        TTo(T.YB[:, 0:256], T.YM[:, :], E[:, 0:256], OP.mult, ["#dB", "YM"], ["YB0"], 256)
        for j in range(1, 5):
            k0 = (j - 1) * 256
            MM(E[:, 256:512], CW[0:8, 1152:1280], NTs(5 + j, 8), True, True, ["wE", "NT%d" % (5 + j)], ["#dB"], 128, 256)
            TS(T.YK[:, k0:k0 + 256], T.YP[:, :], float(j), OP.is_equal, ["YP"], ["YK%d" % j], 128)
            TTo(T.YB[:, 256 + j * 256:512 + j * 256], T.YK[:, k0:k0 + 256], E[:, 256:512], OP.mult, ["YK%d" % j, "#dB"], ["YB%d" % (j + 1)], 256)
        for z in range(6):
            MM(D[:, 0:256], I16, T.YB[:, z * 256:z * 256 + 256], z == 0, z == 5, ["hI", "YB%d" % z], ["#dA"], 128, 256)
        S(T.YR[:, t * 256:t * 256 + 256], D[:, 0:256], FN.Copy, ["#dA"], ["YR%d" % t], 256)
        DMA("y", T.yr[:, t * 256:t * 256 + 256], T.YR[:, t * 256:t * 256 + 256], ["YR%d" % t], [])

    start(0)
    for a in range(5):
        step(0, 0, a, T.TO, "TO")
        step(0, 1, a, T.TP0, "TP0")
    late_constants()
    lesser("EL0", T.TO, "TO")
    lesser("ELn", T.TPn, "TPn")
    rings(0, T.TO, "TO")
    send(6)
    arrive("MKP", "aMK", (r + 2) % n, 7.0, ["MKT"])
    show(0)
    lessen(T.TO, "TO", "MKT", "EL0", T.TO1, "T1q", ("kA", "kB", "xB", "wA"))
    op(None, None, ["T1q%d" % q for q in range(4)], ["TO1"], 0.0, "n")
    start(1)
    lessen(T.TPn, "TPn", "MKP", "ELn", T.TP1, "P1q", ("dB",))
    op(None, None, ["P1q%d" % q for q in range(4)], ["TP1"], 0.0, "n")
    for a in range(5):
        step(1, 0, a, T.TO1, "TO1")
        step(1, 1, a, T.TP1, "TP1")
    lesser("EL1", T.TO1, "TO1")
    rings(1, T.TO1, "TO1")
    show(1)
    lessen(T.TO1, "TO1", "MKT", "EL1", T.TO2, "T2q", ("kA", "kB", "xB", "wA"))
    for qd in range(4):
        DMA("y" if qd % 2 == 0 else "s", T.ye[:, qd * 512:qd * 512 + 512], T.TO2[:, qd * 512:qd * 512 + 512], ["T2q%d" % qd], [])
    for o in ops:
        more = set()
        for d in o["deps"]:
            if ops[d]["kind"] == "n":
                more |= ops[d]["deps"]
            else:
                more.add(d)
        o["deps"] = more
    return ops


def schedule(ops):
    n = len(ops)
    wake, same = 0.12, 0.04
    succ = [[] for _ in range(n)]
    need = [0] * n
    for i, o in enumerate(ops):
        for d in o["deps"]:
            succ[d].append((i, False))
            need[i] += 1
        for d in o["order"]:
            succ[d].append((i, True))
            need[i] += 1
    prio = [0.0] * n
    for i in range(n - 1, -1, -1):
        best = 0.0
        for j, od in succ[i]:
            best = max(best, prio[j] + (0.0 if od else (wake if ops[j]["q"] != ops[i]["q"] else same)))
        prio[i] = best + ops[i]["cost"] + ops[i]["lat"]
    prio = [prio[i] + ops[i]["bon"] for i in range(n)]
    ready, free, order = {}, {}, []
    tready, fin = [0.0] * n, [0.0] * n
    for i in range(n):
        if need[i] == 0:
            ready.setdefault(ops[i]["q"], []).append(i)
    while len(order) < n:
        bq, bt = None, 1e18
        for q in ready:
            for i in ready[q]:
                s = max(free.get(q, 0.0), tready[i])
                if s < bt:
                    bt, bq = s, q
        lst = ready[bq]
        pick, pp = None, -1e9
        for i in lst:
            if max(free.get(bq, 0.0), tready[i]) <= bt + 0.1 and prio[i] > pp:
                pick, pp = i, prio[i]
        lst.remove(pick)
        if not lst:
            del ready[bq]
        o = ops[pick]
        s = max(free.get(bq, 0.0), tready[pick])
        if bq is not None:
            free[bq] = s + o["cost"]
        fin[pick] = s + o["cost"] + o["lat"]
        order.append(pick)
        for j, od in succ[pick]:
            tj = s if od else fin[pick] + (wake if ops[j]["q"] != o["q"] else same)
            tready[j] = max(tready[j], tj)
            need[j] -= 1
            if need[j] == 0:
                ready.setdefault(ops[j]["q"], []).append(j)
    return order


def emit(g, T, ops, order):
    eng = {"v": g.vector, "s": g.scalar, "t": g.tensor, "g": g, "y": g.sync}
    csem = {"v": "v", "s": "s", "t": "t", "g": "gc"}
    count, final = {}, {}
    know = {q: {} for q in eng}
    mark = [None] * len(ops)
    after = [None] * len(ops)
    for i in order:
        o = ops[i]
        q = o["q"]
        if o["kind"] == "n":
            continue
        if o["kind"] == "x":
            mark[i] = (o["sem"], o["val"])
            after[i] = {o["sem"]: o["val"]}
            final[o["sem"]] = o["val"]
            continue
        K = know[q]
        for d in sorted(o["deps"], key=lambda d: -sum(after[d].values())):
            s, v = mark[d]
            if K.get(s, 0) >= v:
                continue
            eng[q].wait_ge(T.sem[s], v)
            for s2, v2 in after[d].items():
                if K.get(s2, 0) < v2:
                    K[s2] = v2
        if q == "g" and o["kind"] == "c" and K.get("gc", 0) < count.get("gc", 0):
            g.wait_ge(T.sem["gc"], count["gc"])
            K["gc"] = count["gc"]
        ins = o["fn"]()
        if o["kind"] == "c":
            s = csem[q]
            count[s] = count.get(s, 0) + 1
            ins.then_inc(T.sem[s], 1)
            mark[i] = (s, count[s])
        elif o["kind"] == "d":
            ins.then_inc(T.sem[o["sem"]], 16)
            mark[i] = (o["sem"], 16)
        else:
            mark[i] = (o["sem"], o["val"])
        final[mark[i][0]] = mark[i][1]
        after[i] = dict(K)
        after[i][mark[i][0]] = mark[i][1]
    for s in final:
        if know["g"].get(s, 0) < final[s]:
            g.wait_ge(T.sem[s], final[s])


def rank_program(g, core, T, topo):
    if T.rank_of(core) is None:
        hand_on(g, core, T, topo)
        return
    ops = build(g, core, T, topo)
    if "order" not in ORDERS:
        ORDERS["order"] = schedule(ops)
    emit(g, T, ops, ORDERS["order"])
